import numpy as np, ml_dtypes
CORES = [83,85,87,115,117,119]
N = 6
BF = ml_dtypes.bfloat16
def gentries(a):
    return np.ascontiguousarray(a.reshape(8, 16, -1).transpose(0, 2, 1)).reshape(8, -1)
def gtable(e):
    e = np.asarray(e); return np.ascontiguousarray(e.reshape(8, -1, 16).transpose(0, 2, 1)).reshape(128, -1).astype(np.int32)
W, L, RO, PE, ES, LAST = 4096, 256, 3, 2, 5, 0
def names(rng): return rng.integers(0, W, (N, 8, L, 16))
def pack(x, s, z):
    return {"cont": np.ascontiguousarray(np.reshape(x, (N, 128, W))).astype(np.float32).astype(BF),
            "enz": np.stack([gtable(a.reshape(8, -1)) for a in s]), "subs": np.stack([gtable(a.reshape(8, -1)) for a in z])}
def setup_inputs(rng):
    x = np.where(rng.random((N, 8, 1, W)) < 0.3, 51 * rng.integers(0, 6, (N, 8, 16, W)), rng.integers(0, 256, (N, 8, 16, W)))
    s, z = names(rng), names(rng); u = rng.random((N, 8, L, 1))
    z = np.where((u < 0.15) & (rng.random(z.shape) < 0.3), s[..., 15:], z)
    z = np.where((u > 0.9) & (rng.random(z.shape) < 0.5), z[..., 7:8], z)
    return pack(x, s, z)
def setup_inputs_spread(rng):
    x = np.minimum((np.exp2(3 + 5.5 * rng.random((N, 8, 1, W))) * rng.random((N, 8, 16, W))).astype(np.int64), 255)
    e = rng.choice(np.array([1.0, 1.5, 2.0, 3.0, 4.0]), (N, 8, 1, 1))
    s = np.minimum((W * rng.random((N, 8, L, 16)) ** e).astype(np.int64), W - 1)
    z = W - 1 - np.minimum((W * rng.random((N, 8, L, 16)) ** e).astype(np.int64), W - 1)
    return pack(x, s, z)
def setup_inputs_ends(rng):
    x = 255 * (rng.random((N, 8, 16, W)) < rng.choice(np.array([0.0, 0.1, 0.3, 0.5, 0.7, 0.9, 1.0]), (N, 8, 1, W)))
    near = (np.arange(16)[:, None] == rng.integers(0, 16, (N, 8, 1, W))) & (rng.random((N, 8, 1, W)) < 0.3)
    x = np.where(near, np.where(x == 0, 1, 254), x)
    m = np.stack([np.concatenate([rng.permutation(np.array([0, 10, 6, 8, 7, 9, 12])), np.array([16])]) for q in range(N)])
    top = np.argsort(rng.random((N, 8, 16)), axis=-1) < m[..., None]
    x[..., W - 1] = np.where(top, 255, 0); x[..., 0] = np.where(top, 0, 255)
    x[:, 7, :, W - 2] = 255; x[:, 7, 15, W - 2] = 254; x[:, 7, :, 1] = 0; x[:, 7, 0, 1] = 1
    x[:, 7, :, W - 3] = 255; x[:, 7, 14:, W - 3] = 254
    sz = []
    for i in range(2):
        fr = rng.choice(np.array([1.0, 0.6]), (N, 8, L, 1))
        sz.append(np.where(rng.random((N, 8, L, 16)) < fr, (W - 1) * rng.integers(0, 2, (N, 8, L, 16)), names(rng)))
    s, z = sz; alt = np.where(np.arange(16) & 1 == 1, W - 1, 0)
    for a, b, c in ((L - 1, L - 2, L - 3), (0, 1, 2)):
        s[:, 7, a] = W - 1 - alt; z[:, 7, a] = W - 1; z[:, 7, a, 9] = W - 2; z[:, 7, a, 15] = W - 2
        s[:, 7, b] = alt; z[:, 7, b] = 0
        s[:, 7, c] = alt; z[:, 7, c] = W - 1
        z[:, 7, c, 5] = W - 31
    for i, (p1, p2) in enumerate(((6, 11), (1, 14), (0, 15))):
        for a in (L - 4 - i, 3 + i):
            s[:, 7, a] = W - 1 - alt; z[:, 7, a] = W - 1; z[:, 7, a, p1] = W - 2; z[:, 7, a, p2] = W - 3
    return pack(x, s, z)
def setup_inputs_corners(rng):
    B = W // 16; kind = rng.integers(0, 7, (N, 8, B))
    for q in range(N):
        g = rng.permutation(8); kind[q, g[0]] = 0; kind[q, g[1]] = 3
    opts = ([0, 2, 4], [0, 2, 4], [5, 7, 9, 11], [6, 7, 8, 9], [10, 11, 12, 13], [5, 6, 7, 9, 10], list(range(17)))
    cs = np.zeros((N, 8, B, 16), np.int64)
    for i, o in enumerate(opts): cs = np.where(kind[..., None] == i, rng.choice(np.array(o), cs.shape), cs)
    cs[..., 0] = np.where(kind == 1, rng.choice(np.array([1, 3, 5]), kind.shape), cs[..., 0])
    down = (np.argsort(rng.random((N, 8, B, 16, 16)), axis=-1) < cs[..., None]).transpose(0, 1, 2, 4, 3).copy()
    down[..., 0] &= ~np.all(down, axis=-1)
    st = rng.integers(1, 17, down.shape); v = np.zeros(down.shape, np.int64); cur = np.full(down.shape[:-1], 255)
    for k in range(32):
        v[..., k & 15] = cur; cur = np.where(down[..., k & 15], cur - st[..., k & 15], 255)
    x = np.ascontiguousarray(v.transpose(0, 1, 3, 2, 4)).reshape(N, 8, 16, W)
    blk = np.concatenate([np.argsort(rng.random((N, 8, B)), axis=-1) for i in range(2)], axis=-1)[..., :L]
    rot = np.where(np.arange(L) < B, 0, rng.integers(0, 16, (N, 8, L)))
    s = 16 * blk[..., None] + ((np.arange(16) + rot[..., None]) & 15)
    inv = np.argsort(rng.random((N, 8, W)), axis=-1); new = np.argsort(inv, axis=-1)
    x = np.take_along_axis(x, inv[:, :, None], 3); s = np.take_along_axis(new, s.reshape(N, 8, -1), 2).reshape(N, 8, L, 16)
    one = rng.choice(np.array([0, W - 1, W // 2, 5]), (N, 8, L, 1)); s = np.where(rng.random((N, 8, L, 1)) < 0.1, one, s)
    z = names(rng); zk = rng.integers(0, 7, (N, 8, L, 1)); p = np.arange(16); own = s[..., 15:]
    z = np.where((zk == 1) & (p == 15), own, z); z = np.where((zk == 2) & ((p == 0) | (p == 15)), own, z)
    z = np.where(zk == 3, own, z); z = np.where(zk == 4, s, z)
    z = np.where(zk == 5, (W - 1) * rng.integers(0, 2, z.shape), z); z = np.where((zk == 6) & (p == rng.integers(0, 16, zk.shape)), own, z)
    return pack(x, s, z)
def setup_inputs_ties(rng):
    lev = np.array([[0, 1, 254, 255], [3, 4, 5, 250]])[np.arange(8) & 1]
    x = np.take_along_axis(np.broadcast_to(lev[None], (N, 8, 4)), rng.integers(0, 4, (N, 8, 16 * W)), 2).reshape(N, 8, 16, W)
    pool = rng.integers(0, W, (N, 8, 24)); pool[..., 0] = 0; pool[..., 1] = W - 1
    s = np.take_along_axis(pool, rng.integers(0, 24, (N, 8, L * 16)), 2).reshape(N, 8, L, 16)
    z = np.take_along_axis(pool, rng.integers(0, 24, (N, 8, L * 16)), 2).reshape(N, 8, L, 16)
    u = rng.random((N, 8, L, 1)); z = np.where(u < 0.2, s, z); z = np.where(u > 0.85, z[..., 3:4], z)
    return pack(x, s, z)
def setup_inputs_full(rng):
    B = W // 16; kind = np.stack([rng.permutation(np.array([0, 0, 0, 1, 1, 2, 2, 2])) for q in range(N)]); kind[0, 7] = 1; kind[N - 1, 7] = 0
    k4 = kind[:, :, None, None]
    cs = np.where(k4 == 0, rng.choice(np.array([10, 12, 14]), (N, 8, B, 16)), rng.integers(6, 16, (N, 8, B, 16)))
    cs[..., 0] += ((kind[:, :, None] == 0) & (rng.random((N, 8, B)) < 0.5)).astype(np.int64)
    t1 = np.argsort(rng.random((N, 8, B, 16)), axis=-1); t2 = np.argsort(rng.random((N, 8, B, 16)), axis=-1)
    down = ((t1[..., :, None] + t2[..., None, :]) & 15) < cs[..., None, :]
    st = rng.integers(1, 17, down.shape); v = np.zeros(down.shape, np.int64); cur = np.full(down.shape[:-1], 255)
    for k in range(32):
        v[..., k & 15] = cur; cur = np.where(down[..., k & 15], cur - st[..., k & 15], 255)
    x = np.ascontiguousarray(v.transpose(0, 1, 3, 2, 4)).reshape(N, 8, 16, W)
    blk = np.concatenate([np.argsort(rng.random((N, 8, B)), axis=-1) for i in range(2)], axis=-1)[..., :L]
    s = 16 * blk[..., None] + np.arange(16)
    inv = np.argsort(rng.random((N, 8, W)), axis=-1); new = np.argsort(inv, axis=-1)
    x = np.take_along_axis(x, inv[:, :, None], 3); s = np.take_along_axis(new, s.reshape(N, 8, -1), 2).reshape(N, 8, L, 16)
    hi = np.arange(W - 96, W); ok = ((hi[:, None] * np.arange(W) >> 5) & (W - 1)) + hi[:, None] + 77 == 2 * W
    made = np.where(np.any(ok, axis=1), np.argmax(ok, axis=1), -1); y = W - 32 + ((-((hi & 31) ** 7)) & 31)
    mate = np.full(W, -1); mate[W - 96:] = np.where(((hi & 1) == 1) & (hi * (y + 32) > 2 ** 24), y, made)
    zu = np.where(mate[s] >= 0, mate[s], names(rng)); zu[..., 0] = s[..., 15]
    way = 1 - 2 * (np.take_along_axis(cs[..., 0], blk, 2) & 1)
    p = (rng.integers(0, 16, (N, 8, L, 1)) + way[..., None] * np.arange(16)) & 15
    z = np.take_along_axis(zu, np.argsort(p, axis=-1), 3)
    z = np.where(rng.random((N, 8, L, 1)) < 0.75, z, names(rng))
    pm = np.argsort(rng.random((N, 8, W)), axis=-1); cl = (np.argsort(pm, axis=-1) >> 9)[:, :, None]
    few = rng.integers(0, 4, (N, 8, 16, W)); x2 = rng.integers(0, 256, (N, 8, 16, W)); x2 = np.where(cl == 0, few, x2)
    for i, b in ((1, 134), (2, 198), (3, 255)): x2 = np.where(cl == i, b - few, x2)
    s2 = names(rng); s2[..., 15] = np.take_along_axis(pm, rng.integers(0, 512, (N, 8, L)), 2)
    zi = 512 * rng.integers(1, 4, (N, 8, L, 1)) + rng.integers(0, 512, (N, 8, L, 16))
    z2 = np.take_along_axis(pm, zi.reshape(N, 8, -1), 2).reshape(N, 8, L, 16)
    return pack(np.where(k4 == 2, x2, x), np.where(k4 == 2, s2, s), np.where(k4 == 2, z2, z))
def check_inputs(d):
    bad = []
    c = np.asarray(d["cont"]).astype(np.float32)
    if not np.all((c >= 0) & (c <= 255)): bad.append("range of cont")
    elif not np.all(c == np.floor(c)): bad.append("whole numbers in cont")
    for k in ("enz", "subs"):
        if np.min(d[k]) < 0 or np.max(d[k]) > W - 1: bad.append("range of " + k)
    return bad
def edit(x, s, z, a, t):
    v = np.take_along_axis(x, s.reshape(8, 1, -1), 2).reshape(8, 16, L, 16)
    y = np.take_along_axis(x, z.reshape(8, 1, -1), 2).reshape(8, 16, L, 16)
    c = np.sum((v > np.roll(v, -1, axis=3)).astype(np.int64), axis=1)
    dist = np.sum(np.abs(y - v[..., 15:16]).astype(np.int64), axis=1)
    step = 1 - 2 * (np.add.accumulate(c, axis=2) & 1); step[..., 0] = np.argmin(dist, axis=2)
    pos = np.add.accumulate(step, axis=2) & 15
    hit = pos[:, :, None, :] == np.arange(16)[:, None]
    e = 15 - np.argmax(hit[..., ::-1], axis=3) if LAST else np.argmax(hit, axis=3)
    has = np.any(hit, axis=3); ce = np.take_along_axis(c, e, 2); se = np.take_along_axis(s, e, 2)
    gone = has & (ce <= 5 + (a & 1)[..., None])
    new = np.where(has, np.where(ce <= 9, se, ((se * z >> 5) + se + 77 * t) & (W - 1)), z)
    n = np.sum(gone.astype(np.int64), axis=2); i = np.arange(16) - (16 - n)[..., None]
    kept = np.take_along_axis(new, np.argsort(gone, axis=2, kind="stable"), 2)
    return np.where(i < 0, kept, np.take_along_axis(s, np.maximum(i, 0), 2)), n
def reference(cont, enz, subs):
    x = cont.astype(np.float32).astype(np.int16).reshape(N, 8, 16, W)
    s = np.stack([gentries(a) for a in enz]).astype(np.int64).reshape(N, 8, L, 16)
    z = np.stack([gentries(a) for a in subs]).astype(np.int64).reshape(N, 8, L, 16)
    dels = np.zeros((N, 8, L), np.int64)
    for t in range(1, RO + 1):
        both = [edit(x[r], s[r], z[r], dels[r], t) for r in range(N)]
        dels = np.stack([b[1] for b in both])
        z = np.roll(s, ES, axis=0)
        s = np.roll(np.stack([b[0] for b in both]), PE, axis=0)
    return {"yenz": np.stack([gtable(a.reshape(8, -1)) for a in s]).astype(np.float32), "ysub": np.stack([gtable(a.reshape(8, -1)) for a in z]).astype(np.float32)}

@@ -1,0 +1,408 @@
+from concourse.mybir import AluOpType as O, ActivationFunctionType as F
+
+NC = 2
+LN = 128
+ROUNDS, HOPP, HOPE = 3, 2, 5
+
+SCRATCH = {
+    "win": ("sbuf", [128, 4096], "bfloat16"),
+    "ei": ("sbuf", [128, 256], "int32"), "zi1": ("sbuf", [128, 256], "int32"),
+    "el": ("sbuf", [128, 256], "uint16"), "zl": ("sbuf", [128, 256], "uint16"),
+    "fo": ("sbuf", [128, 256], "float32"),
+    "V": ("sbuf", [128, 4096], "bfloat16"), "Y": ("sbuf", [128, 4096], "bfloat16"),
+    "cm": ("sbuf", [128, 4096], "bfloat16"), "ab": ("sbuf", [128, 4096], "bfloat16"),
+    "x1": ("sbuf", [128, 512], "float16"), "x2": ("sbuf", [128, 1024], "float16"),
+    "y1": ("sbuf", [128, 8192], "float16"), "y2": ("sbuf", [128, 16384], "float16"),
+    "nc": ("sbuf", [128, 256], "float16"),
+    "M": ("sbuf", [128, 272], "bfloat16"), "m": ("sbuf", [128, 272], "bfloat16"),
+    "sx": ("sbuf", [128, 1280], "int32"), "p0": ("sbuf", [128, 16], "int32"),
+    "Wh": ("sbuf", [128, 2048], "float16"), "Wl": ("sbuf", [128, 2048], "float16"),
+    "idf": ("sbuf", [128, 128], "float16"),
+    "w64": ("sbuf", [128, 8], "float16"), "w1": ("sbuf", [128, 8], "float16"),
+    "b05": ("sbuf", [128, 8], "bfloat16"), "b16": ("sbuf", [128, 8], "bfloat16"),
+    "cc": ("sbuf", [128, 128], "float32"),
+}
+TK = 4
+for _q in range(16 // TK):
+    SCRATCH["D%d" % _q] = ("psum", [128, 128 * TK], "float32")
+for _n in ("st", "si", "s", "par", "km", "t1", "v", "prod", "fl", "sm", "ni", "ai", "thr"):
+    SCRATCH[_n] = ("sbuf", [128, 256], "int32")
+for _n in ("pos", "wp", "wm", "nf", "E1", "E2", "dl", "n32"):
+    SCRATCH[_n] = ("sbuf", [128, 256], "bfloat16")
+for _n in ("i256", "ipark", "i128n", "i65", "iup", "idw", "cb"):
+    SCRATCH[_n] = ("sbuf", [128, 256], "bfloat16")
+for _n in ("id1", "idn", "ones", "bm", "tri",
+           "W2", "W3", "dg2", "dg3", "pio", "pk", "msk", "mmin", "mmax", "tmp", "tmp2"):
+    SCRATCH[_n] = ("sbuf", [128, 128], "bfloat16")
+for _h in range(NC):
+    SCRATCH["KU%d" % _h] = ("psum", [128, 512], "float32")
+    SCRATCH["VP%d" % _h] = ("psum", [128, 512], "float32")
+    SCRATCH["lf%d" % _h] = ("sbuf", [128, LN], "float32")
+    for _t in (2, 3):
+        SCRATCH["le%d%d" % (_t, _h)] = ("sbuf", [128, LN], "uint16")
+        SCRATCH["lz%d%d" % (_t, _h)] = ("sbuf", [128, LN], "uint16")
+    for _t in (2, 3, 4):
+        SCRATCH["lq%d%d" % (_t, _h)] = ("sbuf", [128, LN], "int32" if _t == 2 else "float32")
+    for _t in (1, 2):
+        SCRATCH["po%d%d" % (_t, _h)] = ("sbuf", [128, LN], "uint16")
+        SCRATCH["pf%d%d" % (_t, _h)] = ("sbuf", [128, LN], "float32")
+
+SEMAPHORES = ["cV", "cS", "cP", "cG", "lE", "lZ", "lW", "lW2", "out", "loc"]
+for _h in range(NC):
+    SEMAPHORES += ["aF%d" % _h] + ["a%s%d%d" % (_k, _t, _h) for _k in "EZ" for _t in (2, 3)]
+    SEMAPHORES += ["aQ%d%d" % (_t, _h) for _t in (2, 3, 4)]
+
+CY = 0.00083 * 1.2
+LAG = 3.0
+VFIX, SFIX, PEC, WAKE, LEAD = 0.05, 0.06, 0.00045, 0.14, 6.0
+GATHER = 1.56
+SLACK = {"V": 0.06, "S": 1.0, "P": 0.0, "G": 0.0, "T": 0.0}
+YV = ((1, 0),)
+
+
+def rank_program(g, core, T, topo):
+    rank = T.rank_of(core)
+    if rank is None:
+        return
+    n_ranks = len(T.cores)
+    V, S, P = g.vector, g.scalar, g.tensor
+    ops, cur = [], [0]
+    lastw, readers, bank = {}, {}, {}
+
+    def op(eng, cost, fn, reads=(), writes=(), banks=(), ext=(), after=(), n=1):
+        i = len(ops)
+        deps = set()
+        for r in reads:
+            if r in lastw: deps.add(lastw[r])
+            readers.setdefault(r, []).append(i)
+        for w in writes:
+            if w in lastw and not (eng == "P" and ops[lastw[w]]["e"] == "P"): deps.add(lastw[w])
+            for q in readers.get(w, []):
+                if q != i: deps.add(q)
+            lastw[w] = i
+            readers[w] = []
+        for b in banks:
+            if b not in bank: bank[b] = [eng, [], []]
+            if bank[b][0] != eng: bank[b] = [eng, bank[b][2], []]
+            deps.update(bank[b][1])
+            bank[b][2].append(i)
+        ops.append({"e": eng, "c": cost, "f": fn, "d": deps, "x": list(ext), "a": list(after), "n": n, "h": cur[0]})
+        return i
+
+    def cv(n, rate=1.0):
+        return VFIX + CY * max(64.0, n * rate)
+
+    def ts(out, in0, s1, o0, s2, o1, n, r, w, banks=(), ext=(), rate=1.0):
+        def f():
+            if o1 is None: return [V.tensor_scalar(out, in0, s1, None, o0)]
+            return [V.tensor_scalar(out, in0, s1, s2, o0, o1)]
+        return op("V", cv(n, rate), f, r, w, banks, ext)
+
+    def tt(out, a, b, o, n, r, w, banks=(), ext=(), rate=1.0):
+        return op("V", cv(n, rate), lambda: [V.tensor_tensor(out, a, b, o)], r, w, banks, ext)
+
+    def cp(out, a, n, r, w, banks=(), ext=(), after=(), rate=1.0):
+        return op("V", cv(n, rate), lambda: [V.tensor_copy(out, a)], r, w, banks, ext, after)
+
+    def fill(ap, c, n, w):
+        return op("V", cv(n), lambda: [V.memset(ap, c)], (), w)
+
+    def scan(out, d0, d1, o0, o1, r, w, banks=(), rate=1.0):
+        return op("V", cv(128, rate), lambda: [V.tensor_tensor_scan(out, d0, d1, 0.0, o0, o1)], r, w, banks)
+
+    def act(out, in_, fn, n, r, w, banks=(), bias=0.0, scale=1.0):
+        return op("S", SFIX + CY * n, lambda: [S.activation(out, in_, fn, bias=bias, scale=scale)], r, w, banks)
+
+    def mm(mats, r, w, banks, cyc):
+        return op("P", 0.05 + cyc * PEC, lambda: [P.matmul(o, l, q, a, z) for o, l, q, a, z in mats], r, w, banks, n=len(mats))
+
+    g.sync.dma_start(T.ei[:], T.enz[:]).then_inc(T.sem.lE, 16)
+    g.scalar.dma_start(T.zi1[:], T.subs[:]).then_inc(T.sem.lZ, 16)
+    g.sync.dma_start(T.win[:, 0:2048], T.cont[:, 0:2048]).then_inc(T.sem.lW, 16)
+    g.scalar.dma_start(T.win[:, 2048:4096], T.cont[:, 2048:4096]).then_inc(T.sem.lW2, 16)
+    LE, LZ, LW = [("lE", 16)], [("lZ", 16)], [("lW", 16), ("lW2", 16)]
+    t_load = op("T", 5.0, None)
+    t_names = op("T", 2.5, None)
+
+    fill(T.ones[:], 1.0, 128, ["ones"])
+
+    def asel(out, in_, pat, cmpo, base, cm, r, w):
+        return op("G", 0.5, lambda: [g.affine_select(out, in_, pat, cmpo, 0.0, base, cm)], r, w)
+    asel(T.id1[:], T.ones[:], [[-1, 128]], O.is_equal, 0, 1, ["ones"], ["id1"])
+    asel(T.tmp[:], T.ones[:], [[-16, 8], [0, 16]], O.is_ge, 0, 1, ["ones"], ["tmp"])
+    asel(T.bm[:], T.tmp[:], [[16, 8], [0, 16]], O.is_ge, 15, -1, ["tmp"], ["bm"])
+    asel(T.tri[:], T.bm[:], [[1, 128]], O.is_gt, 0, -1, ["bm"], ["tri"])
+    op("G", 0.5, lambda: [g.iota(T.pio[:], [[0, 8], [1, 16]], 0, 0, allow_small_or_imprecise_dtypes=True)], (), ["pio"])
+    cp(T.el[:], T.ei[:], 256, (), ["el"], ext=LE, after=[(t_names, 0.0)])
+    cp(T.zl[:], T.zi1[:], 256, (), ["zl"], ext=LZ, after=[(t_names, 0.0)])
+    act(T.idn[:], T.id1[:], F.Copy, 128, ["id1"], ["idn"], scale=-1.0)
+    for nm, c, c2 in (("i256", 256.0, 256.0), ("ipark", -8192.0, -8192.0), ("i128n", -128.0, -128.0), ("i65", 65.0, 1.0),
+                      ("iup", 4096.0, 4096.0), ("idw", -4096.0, -4096.0)):
+        act(T[nm][:, 0:128], T.id1[:], F.Copy, 128, ["id1"], [nm], scale=c)
+        act(T[nm][:, 128:256], T.id1[:], F.Copy, 128, ["id1"], [nm], scale=c2)
+    act(T.b05[:], T.bm[:, 0:128:16], F.Copy, 8, ["bm"], ["b05"], scale=0.5)
+    act(T.b16[:], T.bm[:, 0:128:16], F.Copy, 8, ["bm"], ["b16"], scale=16.0)
+    act(T.pk[:], T.pio[:], F.Copy, 128, ["pio"], ["pk"], scale=1.0 / 128)
+    act(T.W3[:], T.bm[:], F.Copy, 128, ["bm"], ["W3"], scale=-64.0)
+    fill(T.msk[:], 1.0, 128, ["msk"])
+    fill(T.msk[:, 0:128:16], 0.0, 8, ["msk"])
+    fill(T.mmin[:], -1.0e6, 128, ["mmin"])
+    fill(T.mmin[:, 0:128:16], 1.0e6, 8, ["mmin"])
+    fill(T.mmax[:], 1.0e6, 128, ["mmax"])
+    fill(T.mmax[:, 0:128:16], -1.0e6, 8, ["mmax"])
+    fill(T.cb[0:64, 0:128], -29.0, 128, ["cb0"])
+    fill(T.cb[0:64, 128:256], -30.0, 128, ["cb1"])
+    fill(T.cb[64:128, :], 1.0 / 64, 256, ["cb2"])
+    fill(T.thr[:], -3, 256, ["thr0", "thr1"])
+    for h in range(NC):
+        fill(T.M[:, 136 * h:136 * h + 1], 99.0, 1, ["Mc%d" % h])
+        fill(T.m[:, 136 * h:136 * h + 1], 0.0, 1, ["mc%d" % h])
+    ts(T.w1[:], T.bm[:, 0:128:16], 1.0, O.mult, None, None, 8, ["bm"], ["w1"])
+    ts(T.w64[:], T.bm[:, 0:128:16], 64.0, O.mult, None, None, 8, ["bm"], ["w64"])
+    fill(T.tmp2[:], 0.0, 128, ["tmp2"])
+    for p in range(16):
+        cp(T.Wl[:, 128 * p:128 * p + 128], T.tmp2[:], 128, ["tmp2"], ["Wl%d" % p], rate=0.5)
+        cp(T.Wl[:, 128 * p + p:128 * p + 128:16], T.bm[:, 0:128:16], 8, ["bm"], ["Wl%d" % p])
+    ts(T.Wh[:], T.Wl[:], 63.0, O.mult, None, None, 2048, ["Wl%d" % p for p in range(16)], ["Wh"], rate=0.5)
+    ts(T.W2[:], T.tri[:], -64.0, O.mult, None, None, 128, ["tri"], ["W2"], rate=0.5)
+    ts(T.dg3[:], T.id1[:], 1024.0, O.mult, None, None, 128, ["id1"], ["dg3"], rate=0.5)
+    tt(T.W2[:], T.W2[:], T.dg3[:], O.add, 128, ["dg3"], ["W2"], rate=2.0)
+    tt(T.tmp[:], T.id1[:], T.pio[:], O.mult, 128, ["id1", "pio"], ["tmp"], rate=2.0)
+    ts(T.dg2[:], T.tmp[:], 64.0, O.mult, None, None, 128, ["tmp"], ["dg2"], rate=0.5)
+    tt(T.dg3[:], T.dg3[:], T.dg2[:], O.add, 128, ["dg2"], ["dg3"], rate=2.0)
+    cp(T.idf[:], T.id1[:], 128, ["id1"], ["idf"], rate=0.5)
+    ts(T.cc[:], T.pio[:], 128960.0, O.mult, 131008.0, O.add, 128, ["pio"], ["cc"])
+
+    n_loc = [0]
+    ARR = 8
+
+    def send(dst_rank, dst, src, sem, r, ext=()):
+        to = T.cores[dst_rank % n_ranks]
+
+        def f():
+            msk = 0
+            for e in topo.engines(core, to)[:ARR]: msk |= 1 << e
+            rid, pid = topo.addr(to)[:2]
+            n_loc[0] += ARR
+            g.remote_dma(dst, src, T.sem[sem], T.sem.loc, pid, rid, msk)
+            return []
+        return op("G", 0.8, f, r, (), ext=ext, n=0)
+
+    sent = {}
+    for h in range(NC):
+        a0, a1 = LN * h, LN * h + LN
+        sent["Z", 2, h] = send(rank + HOPE, T["lz2%d" % h][:], T.el[:, a0:a1], "aZ2%d" % h, ["el"])
+        sent["Q", 2, h] = send(rank + HOPE, T["lq2%d" % h][:], T.ei[:, a0:a1], "aQ2%d" % h, [], LE)
+    dtile = [0]
+
+    def chunk(t, h):
+        K, VP = T["KU%d" % h], T["VP%d" % h]
+        kb, vb = ["KU%d" % h], ["VP%d" % h]
+        a0, a1 = LN * h, LN * h + LN
+        X = lambda nm: T[nm][:, a0:a1]
+        k_ = lambda nm: nm + str(h)
+        ku = lambda q: K[:, 128 * q:128 * q + 128]
+        vp = lambda q: VP[:, 128 * q:128 * q + 128]
+        sx = lambda q, w=1: T.sx[:, 640 * h + 128 * q:640 * h + 128 * (q + w)]
+        if t == 1:
+            elist, zlist, sint, zint = X("el"), X("zl"), X("ei"), X("zi1")
+            er, zr, srd = ["el"], ["zl"], []
+            ex_e, ex_z, ex_si, ex_q = [], [], LE, LZ
+            aft_e, aft_z = [], []
+        else:
+            elist, zlist = T["le%d%d" % (t, h)][:], T["lz%d%d" % (t, h)][:]
+            sint, zint = X("si"), T["lq%d%d" % (t, h)][:]
+            er, zr, srd = [], [], [k_("si")]
+            ex_e, ex_z, ex_q = [[("a%s%d%d" % (k, t, h), ARR)] for k in "EZQ"]
+            ex_si = []
+            aft_e, aft_z = [(sent["E", t, h], LAG)], [(sent["Z", t, h], LAG)]
+
+        def gather(eng, dst, lst, r, w, ext, aft):
+            o_ = T[dst][:, 2048 * h:2048 * h + 2048]
+            w_ = T.win[:, 0:4096].indirect(lst)
+            f = (lambda: [S.activation(o_, w_, F.Copy)]) if eng == "S" else (lambda: [V.tensor_copy(o_, w_)])
+            op(eng, 0.06 + 2048 * GATHER * CY, f, r, w, ext=ext + LW, after=aft + [(t_load, 0.0)])
+        gather("V" if (t, h) in YV else "S", "Y", zlist, zr, [k_("Y")], ex_z, aft_z)
+        gather("S", "V", elist, er, [k_("V")], ex_e, aft_e)
+        if t > 1: cp(sint, elist, 128, er, [k_("si")], ext=ex_e, after=aft_e)
+        ts(sx(3), sint, 6, O.arith_shift_right, None, None, 128, srd, [k_("sh")], ext=ex_si)
+        ts(sx(2), sint, 63, O.bitwise_and, None, None, 128, srd, [k_("sl")], ext=ex_si)
+        tt(sx(4), sx(2), sx(3), O.add, 128, [k_("sl"), k_("sh")], [k_("sb")], rate=2.0)
+
+        vs = lambda nm, k: T[nm][:, 2048 * h + k:2048 * h + 2048:16]
+        for kind in (0, 1):
+            src, dst = (("V", "cm"), ("Y", "ab"))[kind]
+            for half in range(16 // TK):
+                d = "D%d" % (dtile[0] % (16 // TK))
+                dtile[0] += 1
+                D = T[d]
+                mats = []
+                for j in range(TK):
+                    k = TK * half + j
+                    o_ = D[:, 128 * j:128 * j + 128]
+                    mats.append((o_, T.id1[:], vs(src, k), True, False))
+                    mats.append((o_, T.idn[:], vs("V", (k + 1) % 16 if kind == 0 else 15), False, True))
+                mm(mats, ["id1", "idn", k_("V")] + ([k_("Y")] if kind else []), [d], [d], 256 * TK)
+                n = 128 * TK
+                out = T[dst][:, 2048 * h + n * half:2048 * h + n * half + n]
+                act(out, D[:], F.Abs if kind else F.Sign, n, [d], [k_(dst + str(half))], [d], bias=0.0 if kind else -0.5)
+        blk = lambda nm, k: T[nm][:, 2048 * h + 128 * k:2048 * h + 128 * k + 128]
+        for ks, qs in ((range(16 - TK), range(16 // TK - 1)), (range(16 - TK, 16), [16 // TK - 1])):
+            mm([(K[:, k:128:16], blk("cm", k), T.b05[:], True, True) for k in ks],
+               ["b05"] + [k_("cm%d" % q) for q in qs], [k_("k0")], kb, 64 * len(ks))
+        scan(X("s"), T.msk[:], ku(0), O.mult, O.add, ["msk", k_("k0")], [k_("s")], kb)
+        ts(X("par"), X("s"), 1, O.bitwise_and, None, None, 128, [k_("s")], [k_("par")])
+        ts(X("st"), X("par"), -2.0, O.mult, 1.0, O.add, 128, [k_("par")], [k_("st")])
+        tt(X("E1"), ku(0), X("thr"), O.is_gt, 128, [k_("k0"), k_("thr")], [k_("E1")], kb)
+        ts(X("E2"), ku(0), 1.5, O.is_gt, None, None, 128, [k_("k0")], [k_("E2")], kb)
+        mm([(vp(1), T.ones[:], T.pk[:], True, False)] +
+           [(VP[:, 128 + k:256:16], blk("ab", k), T.b16[:], False, False) for k in range(16 - TK)],
+           ["ones", "pk", "b16"] + [k_("ab%d" % q) for q in range(16 // TK - 1)], [k_("A1")], vb, 17 * 64 - 64 * TK)
+        mm([(VP[:, 128 + k:256:16], blk("ab", k), T.b16[:], False, k == 15) for k in range(16 - TK, 16)],
+           ["b16", k_("ab%d" % (16 // TK - 1))], [k_("A1")], vb, 64 * TK)
+        scan(X("km"), T.mmin[:], vp(1), O.max, O.min, ["mmin", k_("A1")], [k_("km")], vb)
+        ts(T.st[:, a0:a1:16], T.km[:, a0 + 15:a1:16], 15, O.bitwise_and, None, None, 8, [k_("km")], [k_("st")])
+        scan(X("pos"), T.msk[:], X("st"), O.mult, O.add, ["msk", k_("st")], [k_("pos")])
+        r0 = 136 * h
+        q1, q0 = (lambda nm: T[nm][:, r0 + 1:r0 + 129]), (lambda nm: T[nm][:, r0:r0 + 128])
+        scan(q1("M"), T.mmax[:], X("pos"), O.min, O.max, ["mmax", k_("pos")], [k_("M")], rate=0.5)
+        scan(q1("m"), T.mmin[:], X("pos"), O.max, O.min, ["mmin", k_("pos")], [k_("m")], rate=0.5)
+        mm([(vp(0), T.id1[:], q1("M"), True, False), (vp(0), T.idn[:], q0("M"), False, False),
+            (vp(0), T.idn[:], q1("m"), False, False), (vp(0), T.id1[:], q0("m"), False, True)],
+           ["id1", "idn", k_("M"), k_("Mc"), k_("m"), k_("mc")], [k_("v0")], vb, 4 * 128)
+        ts(X("wp"), X("pos"), 15.5, O.is_gt, None, None, 128, [k_("pos")], [k_("wp")], rate=0.5)
+        ts(X("wm"), X("pos"), -0.5, O.is_lt, None, None, 128, [k_("pos")], [k_("wm")], rate=0.5)
+        ts(X("nf"), vp(0), 0.0, O.is_equal, None, None, 128, [k_("v0")], [k_("nf")], vb)
+        kw = K[:, 256:512]
+        mm([(kw, T.ones[:], T.cb[:], True, False), (kw, X("E1"), T.i128n[:], False, False), (kw, X("E2"), T.i65[:], False, False),
+            (kw, X("pos"), T.i256[:], False, False), (kw, X("wp"), T.idw[:], False, False), (kw, X("wm"), T.iup[:], False, False)],
+           ["ones", "cb0", "cb1", "cb2", "i128n", "i65", "i256", "idw", "iup", k_("E1"), k_("E2"), k_("pos"), k_("wp"), k_("wm")],
+           [k_("k2"), k_("k3")], kb, 6 * 256)
+        mm([(kw, X("nf"), T.ipark[:], False, True)], ["ipark", k_("nf")], [k_("k2"), k_("k3")], kb, 256)
+        x1 = T.x1[:, 256 * h:256 * h + 256]
+        tt(x1, sx(3, 2), K[:, 256:512], O.add, 256, [k_("k2"), k_("k3"), k_("sh"), k_("sb")], [k_("x1")], kb)
+        for p in range(16):
+            y0 = 4096 * h + 256 * p
+            b = 256.0 * p - 2048.0
+            ts(T.y1[:, y0:y0 + 256], x1, b, O.max, b + 256.0, O.min, 256, [k_("x1")], [k_("y1%d" % p)], rate=0.5)
+            mm([(ku(0), T.Wh[:, 128 * p:128 * p + 128], T.y1[:, y0:y0 + 128], p == 0, False),
+                (ku(0), T.Wl[:, 128 * p:128 * p + 128], T.y1[:, y0 + 128:y0 + 256], False, p == 15)],
+               ["Wh", "Wl%d" % p, k_("y1%d" % p)], [k_("k0")], kb, 256)
+        cp(X("t1"), ku(0), 128, [k_("k0")], [k_("t1")], kb)
+        ts(X("v"), X("t1"), 16383, O.bitwise_and, None, None, 128, [k_("t1")], [k_("v")])
+        ts(X("dl"), X("v"), 12287.5, O.is_gt, None, None, 128, [k_("v")], [k_("dl")])
+        mats = []
+        for q in (2, 3, 0, 1):
+            dg, wt = ((T.dg2, T.W2), (T.dg3, T.W3))[q // 2]
+            mats += [(ku(q), dg[:], T.ones[:], True, False), (ku(q), wt[:], X("dl"), False, True)]
+        mm(mats, ["dg2", "dg3", "W2", "W3", "ones", k_("dl")], [k_("k%d" % q) for q in range(4)], kb, 8 * 128)
+        tt(T.x2[:, 512 * h + 256:512 * h + 512], sx(2, 2), K[:, 256:512], O.add, 256,
+           [k_("k2"), k_("k3"), k_("sl"), k_("sh")], [k_("x3")], kb)
+        ts(vp(1), X("v"), -8192.0, O.add, 0.0, O.max, 128, [k_("v")], [k_("A1")], vb)
+        ts(X("n32"), X("v"), 0.0, O.is_equal, 32.0, O.mult, 128, [k_("v")], [k_("n32")])
+        ts(vp(3), X("v"), 8191.5, O.is_gt, 77.0 * t, O.mult, 128, [k_("v")], [k_("F7")], vb)
+        tt(vp(2), vp(1), X("n32"), O.add, 128, [k_("A1"), k_("n32")], [k_("A")], vb)
+        tt(X("prod"), vp(2), zint, O.mult, 128, [k_("A")], [k_("prod")], vb, ext=ex_q)
+        tt(vp(0), vp(3), X("v"), O.add, 128, [k_("F7"), k_("v")], [k_("v0")], vb)
+        ts(X("fl"), X("prod"), 5, O.arith_shift_right, None, None, 128, [k_("prod")], [k_("fl")])
+        tt(X("sm"), vp(0), X("fl"), O.add, 128, [k_("v0"), k_("fl")], [k_("sm")], vb)
+        ts(sx(0), X("sm"), 6, O.arith_shift_right, 63, O.bitwise_and, 128, [k_("sm")], [k_("nh")])
+        ts(sx(1), X("sm"), 63, O.bitwise_and, None, None, 128, [k_("sm")], [k_("nl")])
+        tt(T.x2[:, 512 * h:512 * h + 256], sx(0, 2), K[:, 0:256], O.add, 256,
+           [k_("k0"), k_("k1"), k_("nh"), k_("nl")], [k_("x2")], kb)
+        if t < ROUNDS:
+            mm([(vp(1), X("dl"), T.bm[:], True, True)], ["bm", k_("dl")], [k_("A1")], vb, 128)
+            cp(X("ni"), vp(1), 128, [k_("A1")], [k_("ni")], vb)
+            ts(X("ai"), X("ni"), 1, O.bitwise_and, None, None, 128, [k_("ni")], [k_("ai")])
+            ts(X("thr"), X("ai"), -3.0, O.add, None, None, 128, [k_("ai")], [k_("thr")])
+        for i in range(16):
+            y0 = 8192 * h + 512 * i
+            ts(T.y2[:, y0:y0 + 512], T.x2[:, 512 * h:512 * h + 512], 64.0 * i, O.max, 64.0 * i + 64.0, O.min, 512,
+               [k_("x2"), k_("x3")], [k_("y2%d" % i)], rate=0.5)
+            o_ = K[:, i:128:16]
+            q = [T.y2[:, y0 + 128 * j:y0 + 128 * j + 128] for j in range(4)]
+            mm([(o_, q[0], T.w64[:], True, False), (o_, q[1], T.w1[:], False, False),
+                (o_, q[2], T.w1[:], False, False), (o_, q[3], T.w64[:], False, True)],
+               ["w64", "w1", k_("y2%d" % i)], [k_("k0")], kb, 256)
+        tt(X("nc"), ku(0), T.cc[:], O.subtract, 128, [k_("k0"), "cc"], [k_("nc")], kb)
+        mm([(ku(1), X("nc"), T.idf[:], True, True)], ["idf", k_("nc")], [k_("k1")], kb, 128)
+        if t < ROUNDS:
+            po, pf = "po%d%d" % (t, h), "pf%d%d" % (t, h)
+            ts(T[po][:], ku(1), 2048.0, O.add, None, None, 128, [k_("k1")], [po], kb)
+            act(T[pf][:], ku(1), F.Identity, 128, [k_("k1")], [pf], kb, bias=2048.0)
+            for kind, t2, hop, src in (("E", t + 1, HOPP, po), ("Z", t + 2, HOPP + HOPE, po), ("Q", t + 2, HOPP + HOPE, pf)):
+                if kind == "Z" and t2 > ROUNDS: continue
+                dst = "l%s%d%d" % (kind.lower(), t2, h)
+                sent[kind, t2, h] = send(rank + hop, T[dst][:], T[src][:], "a%s%d%d" % (kind, t2, h), [src])
+        else:
+            ts(X("fo"), ku(1), 2048.0, O.add, None, None, 128, [k_("k1")], [k_("fo")], kb)
+            send(rank + HOPP, T["lf%d" % h][:], X("fo"), "aF%d" % h, [k_("fo")])
+
+    for t in range(1, ROUNDS + 1):
+        for h in range(NC):
+            cur[0] = h
+            chunk(t, h)
+
+    n = len(ops)
+    succ = [[] for _ in range(n)]
+    npred = [0] * n
+    for i, o in enumerate(ops):
+        for d in o["d"]: succ[d].append((i, 0.0))
+        for d, lag in o["a"]: succ[d].append((i, lag))
+        npred[i] = len(o["d"]) + len(o["a"])
+    tail = [0.0] * n
+    for i in range(n - 1, -1, -1):
+        tail[i] = ops[i]["c"] + max([lag + tail[j] for j, lag in succ[i]] + [0.0])
+    ready = [0.0] * n
+    avail = [i for i in range(n) if npred[i] == 0]
+    free = {}
+    order = []
+    while avail:
+        cand = [(max(ready[i], free.get(ops[i]["e"], 0.0)), i) for i in avail]
+        st, i0 = min(cand)
+        e = ops[i0]["e"]
+        best, st = min((-tail[i] - LEAD * (1 - ops[i]["h"]), i, c) for c, i in cand if ops[i]["e"] == e and c <= st + SLACK[e])[1:]
+        avail.remove(best)
+        o = ops[best]
+        end = st + o["c"]
+        if o["e"] != "T": free[o["e"]] = end
+        order.append(best)
+        for j, lag in succ[best]:
+            ready[j] = max(ready[j], end + lag + WAKE)
+            npred[j] -= 1
+            if npred[j] == 0: avail.append(j)
+
+    queue = {"V": V, "S": S, "P": P, "G": g}
+    sem = {"V": T.sem.cV, "S": T.sem.cS, "P": T.sem.cP, "G": T.sem.cG}
+    count = {"V": 0, "S": 0, "P": 0, "G": 0}
+    known = {e: {} for e in queue}
+    done = {}
+    for i in order:
+        o = ops[i]
+        e = o["e"]
+        if e == "T": continue
+        kn = known[e]
+        for d in sorted(o["d"], key=lambda d: -done[d][1]):
+            e2, c2, snap = done[d]
+            if kn.get(e2, 0) >= c2: continue
+            queue[e].wait_ge(sem[e2], c2)
+            for a, b in snap.items():
+                if kn.get(a, 0) < b: kn[a] = b
+            kn[e2] = c2
+        for nm, val in o["x"]:
+            if kn.get(nm, 0) >= val: continue
+            queue[e].wait_ge(T.sem[nm], val)
+            kn[nm] = val
+        for ins in o["f"]():
+            ins.then_inc(sem[e], 1)
+            count[e] += 1
+        if o["n"]: done[i] = (e, count[e], dict(kn))
+
+    y = g.sync
+    for nm, out, land in (("aQ4%d", T.ysub, "lq4%d"), ("aF%d", T.yenz, "lf%d")):
+        for h in range(NC):
+            y.wait_ge(T.sem[nm % h], ARR)
+            y.dma_start(out[:, LN * h:LN * h + LN], T[land % h][:]).then_inc(T.sem.out, 16)
+    y.wait_ge(T.sem.out, 32 * NC)
+    for e in sem: y.wait_ge(sem[e], count[e])
+    g.wait_ge(T.sem.loc, n_loc[0])

@@ -3,61 +3,57 @@ from concourse.mybir import AluOpType as O, ActivationFunctionType as F
 NC = 2
 LN = 128
 ROUNDS, HOPP, HOPE = 3, 2, 5
+TK = 4
+ND = 3
+CDEL, CKEEP, CPROD = (140, 0), (193, 129), {1: (0, 77), 2: (1, 91), 3: (2, 105)}
 
 SCRATCH = {
     "win": ("sbuf", [128, 4096], "bfloat16"),
-    "ei": ("sbuf", [128, 256], "int32"), "zi1": ("sbuf", [128, 256], "int32"),
-    "el": ("sbuf", [128, 256], "uint16"), "zl": ("sbuf", [128, 256], "uint16"),
-    "fo": ("sbuf", [128, 256], "float32"),
+    "ei": ("sbuf", [128, 256], "int32"), "zi": ("sbuf", [128, 256], "int32"),
+    "el": ("sbuf", [128, 256], "uint16"), "zl": ("sbuf", [128, 256], "uint16"), "lz2": ("sbuf", [128, 256], "uint16"),
     "V": ("sbuf", [128, 4096], "bfloat16"), "Y": ("sbuf", [128, 4096], "bfloat16"),
     "cm": ("sbuf", [128, 4096], "bfloat16"), "ab": ("sbuf", [128, 4096], "bfloat16"),
-    "x1": ("sbuf", [128, 512], "float16"), "x2": ("sbuf", [128, 1024], "float16"),
-    "y1": ("sbuf", [128, 8192], "float16"), "y2": ("sbuf", [128, 16384], "float16"),
-    "nc": ("sbuf", [128, 256], "float16"),
-    "M": ("sbuf", [128, 272], "bfloat16"), "m": ("sbuf", [128, 272], "bfloat16"),
-    "sx": ("sbuf", [128, 1280], "int32"), "p0": ("sbuf", [128, 16], "int32"),
-    "Wh": ("sbuf", [128, 2048], "float16"), "Wl": ("sbuf", [128, 2048], "float16"),
-    "idf": ("sbuf", [128, 128], "float16"),
-    "w64": ("sbuf", [128, 8], "float16"), "w1": ("sbuf", [128, 8], "float16"),
-    "b05": ("sbuf", [128, 8], "bfloat16"), "b16": ("sbuf", [128, 8], "bfloat16"),
-    "cc": ("sbuf", [128, 128], "float32"),
+    "bm": ("sbuf", [128, 8, 16], "bfloat16"), "b05": ("sbuf", [128, 2, 8], "bfloat16"), "b256": ("sbuf", [128, 8], "bfloat16"),
+    "wh": ("sbuf", [128, 3, 8], "float16"), "wl": ("sbuf", [128, 3, 8], "float16"),
+    "cA": ("sbuf", [128, 384], "bfloat16"), "c3": ("sbuf", [128, 4, 128], "bfloat16"), "c77": ("sbuf", [128, 3, 128], "bfloat16"),
+    "cx1": ("sbuf", [128, 3, 2, 128], "float32"), "cx2": ("sbuf", [128, 2, 128], "float32"),
+    "iE1": ("sbuf", [128, 256], "bfloat16"), "iE2": ("sbuf", [128, 3, 256], "bfloat16"), "i256": ("sbuf", [128, 256], "bfloat16"),
+    "wr": ("sbuf", [128, 2, 8, 32], "bfloat16"),
+    "idf": ("sbuf", [128, 128], "float16"), "i64f": ("sbuf", [128, 128], "float16"),
+    "KY": ("psum", [128, 512], "float32"),
 }
-TK = 4
-for _q in range(16 // TK):
+for _q in range(ND):
     SCRATCH["D%d" % _q] = ("psum", [128, 128 * TK], "float32")
-for _n in ("st", "si", "s", "par", "km", "t1", "v", "prod", "fl", "sm", "ni", "ai", "thr"):
-    SCRATCH[_n] = ("sbuf", [128, 256], "int32")
-for _n in ("pos", "wp", "wm", "nf", "E1", "E2", "dl", "n32"):
-    SCRATCH[_n] = ("sbuf", [128, 256], "bfloat16")
-for _n in ("i256", "ipark", "i128n", "i65", "iup", "idw", "cb"):
-    SCRATCH[_n] = ("sbuf", [128, 256], "bfloat16")
-for _n in ("id1", "idn", "ones", "bm", "tri",
-           "W2", "W3", "dg2", "dg3", "pio", "pk", "msk", "mmin", "mmax", "tmp", "tmp2"):
+for _n in ("id1", "idn", "i63n", "i64", "i4160n", "ones", "tmp", "pio", "pk", "msk", "mmin", "mmax"):
     SCRATCH[_n] = ("sbuf", [128, 128], "bfloat16")
 for _h in range(NC):
-    SCRATCH["KU%d" % _h] = ("psum", [128, 512], "float32")
-    SCRATCH["VP%d" % _h] = ("psum", [128, 512], "float32")
-    SCRATCH["lf%d" % _h] = ("sbuf", [128, LN], "float32")
-    for _t in (2, 3):
-        SCRATCH["le%d%d" % (_t, _h)] = ("sbuf", [128, LN], "uint16")
-        SCRATCH["lz%d%d" % (_t, _h)] = ("sbuf", [128, LN], "uint16")
-    for _t in (2, 3, 4):
-        SCRATCH["lq%d%d" % (_t, _h)] = ("sbuf", [128, LN], "int32" if _t == 2 else "float32")
-    for _t in (1, 2):
-        SCRATCH["po%d%d" % (_t, _h)] = ("sbuf", [128, LN], "uint16")
-        SCRATCH["pf%d%d" % (_t, _h)] = ("sbuf", [128, LN], "float32")
+    for _n, _s, _d in (("A", [4, 8, 16], None), ("B", [2, 8, 32], None),
+                       ("R", [128], "bfloat16"), ("Sf", [128], "float16"), ("Zf", [128], "float16"),
+                       ("hE", [3, 8, 16], "bfloat16"), ("st", [128], "bfloat16"), ("w", [128], "bfloat16"),
+                       ("M", [136], "bfloat16"), ("m", [136], "bfloat16"), ("nf", [128], "bfloat16"),
+                       ("km", [128], "int32"), ("p0", [128], "int32"), ("pos", [128], "bfloat16"), ("wn", [128], "bfloat16"),
+                       ("x1", [256], "float16"), ("y1", [4096], "float16"),
+                       ("dl", [136], "bfloat16"), ("ds", [128], "bfloat16"), ("nb", [128], "bfloat16"), ("d16", [128], "bfloat16"), ("hn", [128], "bfloat16"),
+                       ("q", [128], "bfloat16"), ("n32", [128], "bfloat16"), ("a", [128], "float32"),
+                       ("prod", [128], "int32"), ("fl", [128], "int32"), ("sm", [128], "int32"), ("nn", [256], "int32"),
+                       ("x2", [2, 8, 32], "float16"), ("y2", [17 * 256], "float16"),
+                       ("le2", [LN], "uint16"), ("le3", [LN], "uint16"), ("lz3", [LN], "uint16"),
+                       ("ly", [LN], "float32"), ("lf", [LN], "float32"),
+                       ("po1", [LN], "uint16"), ("po2", [LN], "uint16"), ("pf2", [LN], "float32"), ("pf3", [LN], "float32")):
+        SCRATCH["%s_%d" % (_n, _h)] = ("sbuf", [128] + _s, _d) if _d else ("psum", [128] + _s, "float32")
 
-SEMAPHORES = ["cV", "cS", "cP", "cG", "lE", "lZ", "lW", "lW2", "out", "loc"]
+SEMAPHORES = ["cV", "cS", "cP", "cG", "lE", "lZ", "lW", "lW2", "out", "loc", "alz2"]
 for _h in range(NC):
-    SEMAPHORES += ["aF%d" % _h] + ["a%s%d%d" % (_k, _t, _h) for _k in "EZ" for _t in (2, 3)]
-    SEMAPHORES += ["aQ%d%d" % (_t, _h) for _t in (2, 3, 4)]
+    SEMAPHORES += ["a%s_%d" % (_k, _h) for _k in ("le2", "le3", "lz3", "ly", "lf")]
 
-CY = 0.00083 * 1.2
-LAG = 3.0
-VFIX, SFIX, PEC, WAKE, LEAD = 0.05, 0.06, 0.00045, 0.14, 6.0
+CY = 0.00087
+LAG = 2.2
+VFIX, SFIX, PEC, WAKE, LEAD = 0.035, 0.065, 0.00044, 0.12, 7.0
 GATHER = 1.56
-SLACK = {"V": 0.06, "S": 1.0, "P": 0.0, "G": 0.0, "T": 0.0}
-YV = ((1, 0),)
+SLACK = {"V": 0.06, "S": 0.5, "P": 0.0, "G": 0.0, "T": 0.0}
+GP = {"V": 2, "Y": 4}
+ONV = [("V", 1, 0, 1)] + [("Y", 1, 0, _j) for _j in range(4)]
+ONS = ()
 
 
 def rank_program(g, core, T, topo):
@@ -76,267 +72,286 @@ def rank_program(g, core, T, topo):
             if r in lastw: deps.add(lastw[r])
             readers.setdefault(r, []).append(i)
         for w in writes:
-            if w in lastw and not (eng == "P" and ops[lastw[w]]["e"] == "P"): deps.add(lastw[w])
+            if w in lastw: deps.add(lastw[w])
             for q in readers.get(w, []):
                 if q != i: deps.add(q)
             lastw[w] = i
             readers[w] = []
+        keep = set()
         for b in banks:
             if b not in bank: bank[b] = [eng, [], []]
             if bank[b][0] != eng: bank[b] = [eng, bank[b][2], []]
             deps.update(bank[b][1])
+            if eng == "P" and bank[b][2]: keep.add(bank[b][2][-1])
             bank[b][2].append(i)
-        ops.append({"e": eng, "c": cost, "f": fn, "d": deps, "x": list(ext), "a": list(after), "n": n, "h": cur[0]})
+        if eng == "P":
+            keep.update(d for d in deps if ops[d]["e"] == "P")
+            deps = {d for d in deps if ops[d]["e"] != "P"}
+        ops.append({"e": eng, "c": cost, "f": fn, "d": deps, "k": keep, "x": list(ext), "a": list(after), "n": n, "h": cur[0]})
         return i
 
     def cv(n, rate=1.0):
         return VFIX + CY * max(64.0, n * rate)
 
-    def ts(out, in0, s1, o0, s2, o1, n, r, w, banks=(), ext=(), rate=1.0):
+    def ts(out, in0, s1, o0, s2, o1, n, r, w, banks=(), ext=(), after=(), rate=1.0):
         def f():
             if o1 is None: return [V.tensor_scalar(out, in0, s1, None, o0)]
             return [V.tensor_scalar(out, in0, s1, s2, o0, o1)]
-        return op("V", cv(n, rate), f, r, w, banks, ext)
+        return op("V", cv(n, rate), f, r, w, banks, ext, after)
 
-    def tt(out, a, b, o, n, r, w, banks=(), ext=(), rate=1.0):
-        return op("V", cv(n, rate), lambda: [V.tensor_tensor(out, a, b, o)], r, w, banks, ext)
+    def tt(out, a, b, o, n, r, w, banks=()):
+        return op("V", cv(n), lambda: [V.tensor_tensor(out, a, b, o)], r, w, banks)
 
     def cp(out, a, n, r, w, banks=(), ext=(), after=(), rate=1.0):
         return op("V", cv(n, rate), lambda: [V.tensor_copy(out, a)], r, w, banks, ext, after)
 
-    def fill(ap, c, n, w):
-        return op("V", cv(n), lambda: [V.memset(ap, c)], (), w)
+    def fill(ap, c, n, w, rate=0.5):
+        return op("V", cv(n, rate), lambda: [V.memset(ap, c)], (), w)
 
-    def scan(out, d0, d1, o0, o1, r, w, banks=(), rate=1.0):
-        return op("V", cv(128, rate), lambda: [V.tensor_tensor_scan(out, d0, d1, 0.0, o0, o1)], r, w, banks)
+    def scan(out, d0, d1, o0, o1, n, r, w, banks=(), rate=1.0, first=0.0):
+        return op("V", cv(n, rate), lambda: [V.tensor_tensor_scan(out, d0, d1, first, o0, o1)], r, w, banks)
 
     def act(out, in_, fn, n, r, w, banks=(), bias=0.0, scale=1.0):
         return op("S", SFIX + CY * n, lambda: [S.activation(out, in_, fn, bias=bias, scale=scale)], r, w, banks)
 
     def mm(mats, r, w, banks, cyc):
-        return op("P", 0.05 + cyc * PEC, lambda: [P.matmul(o, l, q, a, z) for o, l, q, a, z in mats], r, w, banks, n=len(mats))
+        return op("P", 0.03 + cyc * PEC, lambda: [P.matmul(o, l, q, a, z) for o, l, q, a, z in mats], r, w, banks, n=len(mats))
+
+    def evac(name, out, in_, n, r, w, banks):
+        if name in ONS: return act(out, in_, F.Copy, n, r, w, banks)
+        return cp(out, in_, n, r, w, banks)
 
     g.sync.dma_start(T.ei[:], T.enz[:]).then_inc(T.sem.lE, 16)
-    g.scalar.dma_start(T.zi1[:], T.subs[:]).then_inc(T.sem.lZ, 16)
+    g.scalar.dma_start(T.zi[:], T.subs[:]).then_inc(T.sem.lZ, 16)
     g.sync.dma_start(T.win[:, 0:2048], T.cont[:, 0:2048]).then_inc(T.sem.lW, 16)
     g.scalar.dma_start(T.win[:, 2048:4096], T.cont[:, 2048:4096]).then_inc(T.sem.lW2, 16)
     LE, LZ, LW = [("lE", 16)], [("lZ", 16)], [("lW", 16), ("lW2", 16)]
-    t_load = op("T", 5.0, None)
+    t_load = op("T", 7.5, None)
     t_names = op("T", 2.5, None)
 
     fill(T.ones[:], 1.0, 128, ["ones"])
 
     def asel(out, in_, pat, cmpo, base, cm, r, w):
-        return op("G", 0.5, lambda: [g.affine_select(out, in_, pat, cmpo, 0.0, base, cm)], r, w)
+        return op("G", 0.4, lambda: [g.affine_select(out, in_, pat, cmpo, 0.0, base, cm)], r, w)
+
+    def iota(out, pat, w):
+        return op("G", 0.35, lambda: [g.iota(out, pat, 0, 0, allow_small_or_imprecise_dtypes=True)], (), w)
     asel(T.id1[:], T.ones[:], [[-1, 128]], O.is_equal, 0, 1, ["ones"], ["id1"])
     asel(T.tmp[:], T.ones[:], [[-16, 8], [0, 16]], O.is_ge, 0, 1, ["ones"], ["tmp"])
     asel(T.bm[:], T.tmp[:], [[16, 8], [0, 16]], O.is_ge, 15, -1, ["tmp"], ["bm"])
-    asel(T.tri[:], T.bm[:], [[1, 128]], O.is_gt, 0, -1, ["bm"], ["tri"])
-    op("G", 0.5, lambda: [g.iota(T.pio[:], [[0, 8], [1, 16]], 0, 0, allow_small_or_imprecise_dtypes=True)], (), ["pio"])
+    iota(T.pio[:], [[32, 8], [1, 16]], ["pio"])
     cp(T.el[:], T.ei[:], 256, (), ["el"], ext=LE, after=[(t_names, 0.0)])
-    cp(T.zl[:], T.zi1[:], 256, (), ["zl"], ext=LZ, after=[(t_names, 0.0)])
-    act(T.idn[:], T.id1[:], F.Copy, 128, ["id1"], ["idn"], scale=-1.0)
-    for nm, c, c2 in (("i256", 256.0, 256.0), ("ipark", -8192.0, -8192.0), ("i128n", -128.0, -128.0), ("i65", 65.0, 1.0),
-                      ("iup", 4096.0, 4096.0), ("idw", -4096.0, -4096.0)):
-        act(T[nm][:, 0:128], T.id1[:], F.Copy, 128, ["id1"], [nm], scale=c)
-        act(T[nm][:, 128:256], T.id1[:], F.Copy, 128, ["id1"], [nm], scale=c2)
-    act(T.b05[:], T.bm[:, 0:128:16], F.Copy, 8, ["bm"], ["b05"], scale=0.5)
-    act(T.b16[:], T.bm[:, 0:128:16], F.Copy, 8, ["bm"], ["b16"], scale=16.0)
+    cp(T.zl[:], T.zi[:], 256, (), ["zl"], ext=LZ, after=[(t_names, 0.0)])
+
+    def diag(out, c, w, eng="S"):
+        if eng == "S": act(out, T.id1[:], F.Copy, 128, ["id1"], [w], scale=c)
+        else: ts(out, T.id1[:], c, O.mult, None, None, 128, ["id1"], [w], rate=0.5)
+    diag(T.idn[:], -1.0, "idn")
+    for j in range(2):
+        half = slice(128 * j, 128 * j + 128)
+        diag(T.i256[:, half], 256.0, "i256%d" % j)
+        diag(T.iE1[:, half], (CKEEP[j] - CDEL[j]) / 32, "iE1%d" % j)
+        for t in range(1, ROUNDS + 1):
+            diag(T.iE2[:, t - 1, half], (CPROD[t][j] - CKEEP[j]) / 32, "iE2%d%d" % (t, j))
+        act(T.b05[:, j], T.bm[:, :, 0], F.Copy, 8, ["bm"], ["b05%d" % j], scale=0.5)
+    for nm, c in (("i63n", -63.0), ("i64", 64.0), ("i4160n", -4160.0)):
+        diag(T[nm][:], c, nm)
+    diag(T.idf[:], 1.0, "idf", "V")
+    diag(T.i64f[:], 64.0, "i64f", "V")
+    act(T.b256[:], T.bm[:, :, 0], F.Copy, 8, ["bm"], ["b256"], scale=256.0)
     act(T.pk[:], T.pio[:], F.Copy, 128, ["pio"], ["pk"], scale=1.0 / 128)
-    act(T.W3[:], T.bm[:], F.Copy, 128, ["bm"], ["W3"], scale=-64.0)
-    fill(T.msk[:], 1.0, 128, ["msk"])
-    fill(T.msk[:, 0:128:16], 0.0, 8, ["msk"])
-    fill(T.mmin[:], -1.0e6, 128, ["mmin"])
-    fill(T.mmin[:, 0:128:16], 1.0e6, 8, ["mmin"])
-    fill(T.mmax[:], 1.0e6, 128, ["mmax"])
-    fill(T.mmax[:, 0:128:16], -1.0e6, 8, ["mmax"])
-    fill(T.cb[0:64, 0:128], -29.0, 128, ["cb0"])
-    fill(T.cb[0:64, 128:256], -30.0, 128, ["cb1"])
-    fill(T.cb[64:128, :], 1.0 / 64, 256, ["cb2"])
-    fill(T.thr[:], -3, 256, ["thr0", "thr1"])
+    for j, c in enumerate((63.0, -1.0, 63.0)):
+        ts(T.wh[:, j], T.bm[:, :, 0], c, O.mult, None, None, 8, ["bm"], ["wh%d" % j])
+        ts(T.wl[:, j], T.bm[:, :, 0], 1.0, O.mult, None, None, 8, ["bm"], ["wl%d" % j])
+    fill(T.wr[:, :, :, 0:16], 0.0, 256, ["wr"])
+    act(T.wr[:, 0, :, 16:32], T.id1[:], F.Copy, 128, ["id1"], ["wr0"])
+    act(T.wr[:, 1, :, 16:32], T.id1[:], F.Copy, 128, ["id1"], ["wr1"], scale=-64.0)
+    for nm, c, c0 in (("msk", 1.0, 0.0), ("mmin", -1.0e7, 1.0e7), ("mmax", 1.0e7, -1.0e7)):
+        fill(T[nm][:], c, 128, [nm])
+        fill(T[nm][:, 0:128:16], c0, 8, [nm])
+    for j, (big, small) in enumerate(((768, 3.0), (3840, 16.5), (4096, 14.5))):
+        fill(T.cA[0:64, 128 * j:128 * j + 128], big / 64, 128, ["cA%d" % j])
+        fill(T.cA[64:128, 128 * j:128 * j + 128], small / 64, 128, ["cA%d" % (j + 3)])
+    fill(T.cA[64:128, 0:128:16], 4.0 / 64, 8, ["cA3"])
+    CA = ["cA%d" % j for j in range(6)]
+    fill(T.c3[:, 0:2], 0.0, 256, ["c30"])
+    fill(T.c3[:, 3], 16.0, 128, ["c31"])
+    iota(T.c3[:, 2], [[0, 8], [-2048, 16]], ["c32"])
+    ts(T.c3[:, 2], T.c3[:, 2], 40960.0, O.add, None, None, 128, ["c32"], ["c32"], rate=0.5)
+    for t in range(1, ROUNDS + 1):
+        fill(T.c77[:, t - 1], -77.0 * t / 128, 128, ["c77%d" % t])
+        for j, s in enumerate((-160, 12128)):
+            c = 256 * 2112 - 2048 + s + CDEL[j] - 128 * (CPROD[t][j] - CDEL[j])
+            fill(T.cx1[:, t - 1, j], float(c), 128, ["cx1%d%d" % (t, j)], rate=1.0)
+    fill(T.cx2[:, 0], -160.0, 128, ["cx20"], rate=1.0)
+    fill(T.cx2[:, 1], 12288.0, 128, ["cx21"], rate=1.0)
     for h in range(NC):
-        fill(T.M[:, 136 * h:136 * h + 1], 99.0, 1, ["Mc%d" % h])
-        fill(T.m[:, 136 * h:136 * h + 1], 0.0, 1, ["mc%d" % h])
-    ts(T.w1[:], T.bm[:, 0:128:16], 1.0, O.mult, None, None, 8, ["bm"], ["w1"])
-    ts(T.w64[:], T.bm[:, 0:128:16], 64.0, O.mult, None, None, 8, ["bm"], ["w64"])
-    fill(T.tmp2[:], 0.0, 128, ["tmp2"])
-    for p in range(16):
-        cp(T.Wl[:, 128 * p:128 * p + 128], T.tmp2[:], 128, ["tmp2"], ["Wl%d" % p], rate=0.5)
-        cp(T.Wl[:, 128 * p + p:128 * p + 128:16], T.bm[:, 0:128:16], 8, ["bm"], ["Wl%d" % p])
-    ts(T.Wh[:], T.Wl[:], 63.0, O.mult, None, None, 2048, ["Wl%d" % p for p in range(16)], ["Wh"], rate=0.5)
-    ts(T.W2[:], T.tri[:], -64.0, O.mult, None, None, 128, ["tri"], ["W2"], rate=0.5)
-    ts(T.dg3[:], T.id1[:], 1024.0, O.mult, None, None, 128, ["id1"], ["dg3"], rate=0.5)
-    tt(T.W2[:], T.W2[:], T.dg3[:], O.add, 128, ["dg3"], ["W2"], rate=2.0)
-    tt(T.tmp[:], T.id1[:], T.pio[:], O.mult, 128, ["id1", "pio"], ["tmp"], rate=2.0)
-    ts(T.dg2[:], T.tmp[:], 64.0, O.mult, None, None, 128, ["tmp"], ["dg2"], rate=0.5)
-    tt(T.dg3[:], T.dg3[:], T.dg2[:], O.add, 128, ["dg2"], ["dg3"], rate=2.0)
-    cp(T.idf[:], T.id1[:], 128, ["id1"], ["idf"], rate=0.5)
-    ts(T.cc[:], T.pio[:], 128960.0, O.mult, 131008.0, O.add, 128, ["pio"], ["cc"])
+        for nm, ap, c, n, rate in (("M", T["M_%d" % h][:, 0:1], 99.0, 1, 1), ("m", T["m_%d" % h][:, 0:1], 0.0, 1, 1),
+                                   ("p0", T["p0_%d" % h][:], -1000, 128, 1),
+                                   ("dl", T["dl_%d" % h][:, 0:1], 0.0, 1, 1), ("nb", T["nb_%d" % h][:], 0.0, 128, 0.5),
+                                   ("hn", T["hn_%d" % h][:], 258.0, 128, 0.5)):
+            fill(ap, c, n, [nm + str(h)], rate)
 
     n_loc = [0]
     ARR = 8
+    sent = {}
 
-    def send(dst_rank, dst, src, sem, r, ext=()):
-        to = T.cores[dst_rank % n_ranks]
+    def send(hop, dst, src, r):
+        to = T.cores[(rank + hop) % n_ranks]
 
         def f():
             msk = 0
             for e in topo.engines(core, to)[:ARR]: msk |= 1 << e
             rid, pid = topo.addr(to)[:2]
             n_loc[0] += ARR
-            g.remote_dma(dst, src, T.sem[sem], T.sem.loc, pid, rid, msk)
+            g.remote_dma(T[dst][:], src, T.sem["a" + dst], T.sem.loc, pid, rid, msk)
             return []
-        return op("G", 0.8, f, r, (), ext=ext, n=0)
+        sent[dst] = op("G", 0.4, f, r, (), n=0)
 
-    sent = {}
-    for h in range(NC):
-        a0, a1 = LN * h, LN * h + LN
-        sent["Z", 2, h] = send(rank + HOPE, T["lz2%d" % h][:], T.el[:, a0:a1], "aZ2%d" % h, ["el"])
-        sent["Q", 2, h] = send(rank + HOPE, T["lq2%d" % h][:], T.ei[:, a0:a1], "aQ2%d" % h, [], LE)
+    send(HOPE, "lz2", T.el[:], ["el"])
     dtile = [0]
 
     def chunk(t, h):
-        K, VP = T["KU%d" % h], T["VP%d" % h]
-        kb, vb = ["KU%d" % h], ["VP%d" % h]
+        X = lambda nm: T["%s_%d" % (nm, h)]
+        k_ = lambda *nms: [nm + str(h) for nm in nms]
+        A, B, KY = X("A"), X("B"), T.KY
+        ab, bb, kb = k_("A"), k_("B"), ["KY"]
         a0, a1 = LN * h, LN * h + LN
-        X = lambda nm: T[nm][:, a0:a1]
-        k_ = lambda nm: nm + str(h)
-        ku = lambda q: K[:, 128 * q:128 * q + 128]
-        vp = lambda q: VP[:, 128 * q:128 * q + 128]
-        sx = lambda q, w=1: T.sx[:, 640 * h + 128 * q:640 * h + 128 * (q + w)]
-        if t == 1:
-            elist, zlist, sint, zint = X("el"), X("zl"), X("ei"), X("zi1")
-            er, zr, srd = ["el"], ["zl"], []
-            ex_e, ex_z, ex_si, ex_q = [], [], LE, LZ
-            aft_e, aft_z = [], []
-        else:
-            elist, zlist = T["le%d%d" % (t, h)][:], T["lz%d%d" % (t, h)][:]
-            sint, zint = X("si"), T["lq%d%d" % (t, h)][:]
-            er, zr, srd = [], [], [k_("si")]
-            ex_e, ex_z, ex_q = [[("a%s%d%d" % (k, t, h), ARR)] for k in "EZQ"]
-            ex_si = []
-            aft_e, aft_z = [(sent["E", t, h], LAG)], [(sent["Z", t, h], LAG)]
 
-        def gather(eng, dst, lst, r, w, ext, aft):
-            o_ = T[dst][:, 2048 * h:2048 * h + 2048]
-            w_ = T.win[:, 0:4096].indirect(lst)
+        def landed(nm):
+            if nm in ("el", "zl"): return T[nm], a0, [nm], [], []
+            if nm == "lz2": return T.lz2, a0, [], [("alz2", ARR)], [(sent[nm], LAG)]
+            nm = "%s_%d" % (nm, h)
+            return T[nm], 0, [], [("a" + nm, ARR)], [(sent[nm], LAG)]
+        eb, e0, er, ex, ea = landed("el" if t == 1 else "le%d" % t)
+        zb, z0, zr, zx, za = landed("zl" if t == 1 else "lz%d" % t)
+        el, zl = eb[:, e0:e0 + LN], zb[:, z0:z0 + LN]
+
+        def gather(dst, buf, c0, j, r, ext, aft):
+            n = LN // GP[dst]
+            o_ = T[dst][:, 2048 * h + 16 * n * j:2048 * h + 16 * n * (j + 1)]
+            w_ = T.win[:, 0:4096].indirect(buf[:, c0 + n * j:c0 + n * (j + 1)])
+            eng = "V" if (dst, t, h, j) in ONV else "S"
             f = (lambda: [S.activation(o_, w_, F.Copy)]) if eng == "S" else (lambda: [V.tensor_copy(o_, w_)])
-            op(eng, 0.06 + 2048 * GATHER * CY, f, r, w, ext=ext + LW, after=aft + [(t_load, 0.0)])
-        gather("V" if (t, h) in YV else "S", "Y", zlist, zr, [k_("Y")], ex_z, aft_z)
-        gather("S", "V", elist, er, [k_("V")], ex_e, aft_e)
-        if t > 1: cp(sint, elist, 128, er, [k_("si")], ext=ex_e, after=aft_e)
-        ts(sx(3), sint, 6, O.arith_shift_right, None, None, 128, srd, [k_("sh")], ext=ex_si)
-        ts(sx(2), sint, 63, O.bitwise_and, None, None, 128, srd, [k_("sl")], ext=ex_si)
-        tt(sx(4), sx(2), sx(3), O.add, 128, [k_("sl"), k_("sh")], [k_("sb")], rate=2.0)
+            op(eng, 0.06 + 16 * n * GATHER * CY, f, r, k_(dst + "p%d" % j), ext=ext + LW, after=aft + [(t_load, 0.0)])
+        for j in range(GP["Y"]): gather("Y", zb, z0, j, zr, zx, za)
+        for j in range(GP["V"]): gather("V", eb, e0, j, er, ex, ea)
+        got = lambda nm: k_(*[nm + "p%d" % j for j in range(GP[nm])])
+        ts(X("R")[:], el, 1.0 / 64, O.mult, 159.5078125, O.add, 128, er, k_("R"), ext=ex, after=ea, rate=0.5)
+        ts(X("Sf")[:], el, -2048.0, O.add, None, None, 128, er, k_("Sf"), ext=ex, after=ea, rate=0.5)
+        ts(X("Zf")[:], zl, -2048.0, O.add, None, None, 128, zr, k_("Zf"), ext=zx, after=za, rate=0.5)
 
         vs = lambda nm, k: T[nm][:, 2048 * h + k:2048 * h + 2048:16]
-        for kind in (0, 1):
-            src, dst = (("V", "cm"), ("Y", "ab"))[kind]
-            for half in range(16 // TK):
-                d = "D%d" % (dtile[0] % (16 // TK))
-                dtile[0] += 1
-                D = T[d]
-                mats = []
-                for j in range(TK):
-                    k = TK * half + j
-                    o_ = D[:, 128 * j:128 * j + 128]
-                    mats.append((o_, T.id1[:], vs(src, k), True, False))
-                    mats.append((o_, T.idn[:], vs("V", (k + 1) % 16 if kind == 0 else 15), False, True))
-                mm(mats, ["id1", "idn", k_("V")] + ([k_("Y")] if kind else []), [d], [d], 256 * TK)
-                n = 128 * TK
-                out = T[dst][:, 2048 * h + n * half:2048 * h + n * half + n]
-                act(out, D[:], F.Abs if kind else F.Sign, n, [d], [k_(dst + str(half))], [d], bias=0.0 if kind else -0.5)
         blk = lambda nm, k: T[nm][:, 2048 * h + 128 * k:2048 * h + 128 * k + 128]
-        for ks, qs in ((range(16 - TK), range(16 // TK - 1)), (range(16 - TK, 16), [16 // TK - 1])):
-            mm([(K[:, k:128:16], blk("cm", k), T.b05[:], True, True) for k in ks],
-               ["b05"] + [k_("cm%d" % q) for q in qs], [k_("k0")], kb, 64 * len(ks))
-        scan(X("s"), T.msk[:], ku(0), O.mult, O.add, ["msk", k_("k0")], [k_("s")], kb)
-        ts(X("par"), X("s"), 1, O.bitwise_and, None, None, 128, [k_("s")], [k_("par")])
-        ts(X("st"), X("par"), -2.0, O.mult, 1.0, O.add, 128, [k_("par")], [k_("st")])
-        tt(X("E1"), ku(0), X("thr"), O.is_gt, 128, [k_("k0"), k_("thr")], [k_("E1")], kb)
-        ts(X("E2"), ku(0), 1.5, O.is_gt, None, None, 128, [k_("k0")], [k_("E2")], kb)
-        mm([(vp(1), T.ones[:], T.pk[:], True, False)] +
-           [(VP[:, 128 + k:256:16], blk("ab", k), T.b16[:], False, False) for k in range(16 - TK)],
-           ["ones", "pk", "b16"] + [k_("ab%d" % q) for q in range(16 // TK - 1)], [k_("A1")], vb, 17 * 64 - 64 * TK)
-        mm([(VP[:, 128 + k:256:16], blk("ab", k), T.b16[:], False, k == 15) for k in range(16 - TK, 16)],
-           ["b16", k_("ab%d" % (16 // TK - 1))], [k_("A1")], vb, 64 * TK)
-        scan(X("km"), T.mmin[:], vp(1), O.max, O.min, ["mmin", k_("A1")], [k_("km")], vb)
-        ts(T.st[:, a0:a1:16], T.km[:, a0 + 15:a1:16], 15, O.bitwise_and, None, None, 8, [k_("km")], [k_("st")])
-        scan(X("pos"), T.msk[:], X("st"), O.mult, O.add, ["msk", k_("st")], [k_("pos")])
-        r0 = 136 * h
-        q1, q0 = (lambda nm: T[nm][:, r0 + 1:r0 + 129]), (lambda nm: T[nm][:, r0:r0 + 128])
-        scan(q1("M"), T.mmax[:], X("pos"), O.min, O.max, ["mmax", k_("pos")], [k_("M")], rate=0.5)
-        scan(q1("m"), T.mmin[:], X("pos"), O.max, O.min, ["mmin", k_("pos")], [k_("m")], rate=0.5)
-        mm([(vp(0), T.id1[:], q1("M"), True, False), (vp(0), T.idn[:], q0("M"), False, False),
-            (vp(0), T.idn[:], q1("m"), False, False), (vp(0), T.id1[:], q0("m"), False, True)],
-           ["id1", "idn", k_("M"), k_("Mc"), k_("m"), k_("mc")], [k_("v0")], vb, 4 * 128)
-        ts(X("wp"), X("pos"), 15.5, O.is_gt, None, None, 128, [k_("pos")], [k_("wp")], rate=0.5)
-        ts(X("wm"), X("pos"), -0.5, O.is_lt, None, None, 128, [k_("pos")], [k_("wm")], rate=0.5)
-        ts(X("nf"), vp(0), 0.0, O.is_equal, None, None, 128, [k_("v0")], [k_("nf")], vb)
-        kw = K[:, 256:512]
-        mm([(kw, T.ones[:], T.cb[:], True, False), (kw, X("E1"), T.i128n[:], False, False), (kw, X("E2"), T.i65[:], False, False),
-            (kw, X("pos"), T.i256[:], False, False), (kw, X("wp"), T.idw[:], False, False), (kw, X("wm"), T.iup[:], False, False)],
-           ["ones", "cb0", "cb1", "cb2", "i128n", "i65", "i256", "idw", "iup", k_("E1"), k_("E2"), k_("pos"), k_("wp"), k_("wm")],
-           [k_("k2"), k_("k3")], kb, 6 * 256)
-        mm([(kw, X("nf"), T.ipark[:], False, True)], ["ipark", k_("nf")], [k_("k2"), k_("k3")], kb, 256)
-        x1 = T.x1[:, 256 * h:256 * h + 256]
-        tt(x1, sx(3, 2), K[:, 256:512], O.add, 256, [k_("k2"), k_("k3"), k_("sh"), k_("sb")], [k_("x1")], kb)
+
+        def diffs(kind, part):
+            src, dst = (("V", "cm"), ("Y", "ab"))[kind]
+            d = "D%d" % (dtile[0] % ND)
+            dtile[0] += 1
+            D = T[d]
+            mats = []
+            for j in range(TK):
+                k = TK * part + j
+                o_ = D[:, 128 * j:128 * j + 128]
+                mats.append((o_, T.id1[:], vs(src, k), True, False))
+                mats.append((o_, T.idn[:], vs("V", (k + 1) % 16 if kind == 0 else 15), False, True))
+            mm(mats, ["id1", "idn"] + got("V") + (got("Y") if kind else []), [d], [d], 256 * TK)
+            n = 128 * TK
+            out = T[dst][:, 2048 * h + n * part:2048 * h + n * part + n]
+            act(out, D[:], F.Abs if kind else F.Sign, n, [d], k_(dst + str(part)), [d], bias=0.0 if kind else -0.5)
+
+        mm([(A[:, 0:3], T.ones[:], T.cA[:], True, False), (A[:, 1], T.idn[:], X("nb")[:], False, False),
+            (A[:, 1], T.id1[:], X("hn")[:], False, False)], ["ones", "id1", "idn"] + CA + k_("nb", "hn"), k_("cnt"), ab, 640)
+        for part in range(16 // TK):
+            diffs(0, part)
+            mats = []
+            for k in range(TK * part, TK * part + TK):
+                mats += [(A[:, 0, :, max(k, 1):16], blk("cm", k), T.bm[:, :, max(k, 1):16], False, False),
+                         (A[:, 1:3, :, k], blk("cm", k), T.b05[:], False, k == 15)]
+            mm(mats, ["bm", "b050", "b051"] + k_("cm%d" % part), k_("cnt"), ab,
+               sum(64 + max(64, 8 * (16 - k)) for k in range(TK * part, TK * part + TK)))
+        hE = X("hE")
+        evac("hE", hE[:], A[:, 0:3], 384, k_("cnt"), k_("hE"), ab)
+        tt(X("st")[:], hE[:, 0], A[:, 0], O.subtract, 128, k_("cnt", "hE"), k_("st"), ab)
+        scan(X("w")[:], T.msk[:], X("st")[:], O.mult, O.add, 128, ["msk"] + k_("st"), k_("w"), rate=0.5)
+        q1, q0 = (lambda nm: X(nm)[:, 1:129]), (lambda nm: X(nm)[:, 0:128])
+        scan(q1("M"), T.mmax[:], X("w")[:], O.min, O.max, 128, ["mmax"] + k_("w"), k_("M"), rate=0.5)
+        scan(q1("m"), T.mmin[:], X("w")[:], O.max, O.min, 128, ["mmin"] + k_("w"), k_("m"), rate=0.5)
+        mm([(A[:, 3], T.id1[:], q1("M"), True, False), (A[:, 3], T.idn[:], q0("M"), False, False),
+            (A[:, 3], T.idn[:], q1("m"), False, False), (A[:, 3], T.id1[:], q0("m"), False, True)],
+           ["id1", "idn"] + k_("M", "m"), k_("dr"), ab, 4 * 128)
+        ts(X("nf")[:], A[:, 3], 0.0, O.is_equal, -32.0, O.mult, 128, k_("dr"), k_("nf"), ab)
+        mm([(KY[:, a0:a1], T.ones[:], T.pk[:], True, False)], ["ones", "pk"], k_("key"), kb, 128)
+        for part in range(16 // TK):
+            diffs(1, part)
+            mm([(KY[:, a0 + k:a1:16], blk("ab", k), T.b256[:], False, k == 15) for k in range(TK * part, TK * part + TK)],
+               ["b256"] + k_("ab%d" % part), k_("key"), kb, 64 * TK)
+        scan(X("km")[:], T.mmin[:], KY[:, a0:a1], O.max, O.min, 128, ["mmin"] + k_("key"), k_("km"), kb)
+        ts(X("p0")[:, 0:128:16], X("km")[:, 15:128:16], 255, O.bitwise_and, None, None, 8, k_("km"), k_("p0"))
+        scan(X("pos")[:], X("p0")[:], X("st")[:], O.max, O.add, 128, k_("p0", "st"), k_("pos"), first=-1000.0)
+        ts(X("wn")[:], X("pos")[:], -1.0, O.mult, -2104.5, O.add, 128, k_("pos"), k_("wn"), rate=0.5)
+        xw = B[:, 0]
+        xh, xl = B[:, 0, 0:4], B[:, 0, 4:8]
+        mm([(xw, hE[:, 1], T.iE1[:], True, False), (xw, hE[:, 2], T.iE2[:, t - 1], False, False),
+            (xh, T.id1[:], X("R")[:], False, False), (xl, T.i63n[:], X("R")[:], False, False),
+            (xl, T.idf[:], X("Sf")[:], False, False)],
+           ["iE10", "iE11", "iE2%d0" % t, "iE2%d1" % t, "id1", "i63n", "idf"] + k_("hE", "R", "Sf"), k_("xp"), bb, 7 * 128)
+        for nm in ("nf", "pos", "wn"):
+            mm([(xw, X(nm)[:], T.i256[:], False, nm == "wn")], ["i2560", "i2561"] + k_(nm), k_("xp"), bb, 256)
+        tt(X("x1")[:], xw, T.cx1[:, t - 1], O.add, 256, k_("xp") + ["cx1%d0" % t, "cx1%d1" % t], k_("x1"), bb)
+        mm([(A[:], T.ones[:], T.c3[:], True, False), (A[:, 2], T.ones[:], T.c77[:, t - 1], False, False),
+            (A[:, 3], X("Zf")[:], T.idf[:], False, False)],
+           ["ones", "c30", "c31", "c32", "c77%d" % t, "idf"] + k_("Zf"), k_("T"), ab, 768)
+        mm([(B[:], X("R")[:], T.wr[:], True, False), (B[:, 1, :, 16:32], X("Sf")[:], T.idf[:], False, False)],
+           ["wr", "wr0", "wr1", "idf"] + k_("R", "Sf"), k_("xq"), bb, 640)
+        y1 = X("y1")
         for p in range(16):
-            y0 = 4096 * h + 256 * p
             b = 256.0 * p - 2048.0
-            ts(T.y1[:, y0:y0 + 256], x1, b, O.max, b + 256.0, O.min, 256, [k_("x1")], [k_("y1%d" % p)], rate=0.5)
-            mm([(ku(0), T.Wh[:, 128 * p:128 * p + 128], T.y1[:, y0:y0 + 128], p == 0, False),
-                (ku(0), T.Wl[:, 128 * p:128 * p + 128], T.y1[:, y0 + 128:y0 + 256], False, p == 15)],
-               ["Wh", "Wl%d" % p, k_("y1%d" % p)], [k_("k0")], kb, 256)
-        cp(X("t1"), ku(0), 128, [k_("k0")], [k_("t1")], kb)
-        ts(X("v"), X("t1"), 16383, O.bitwise_and, None, None, 128, [k_("t1")], [k_("v")])
-        ts(X("dl"), X("v"), 12287.5, O.is_gt, None, None, 128, [k_("v")], [k_("dl")])
+            ts(y1[:, 256 * p:256 * p + 256], X("x1")[:], b, O.max, b + 256.0, O.min, 256, k_("x1"), k_("y1%d" % p), rate=0.5)
+            mm([(A[:, 0:3, :, p], y1[:, 256 * p:256 * p + 128], T.wh[:], False, False),
+                (A[:, 0:3, :, p], y1[:, 256 * p + 128:256 * p + 256], T.wl[:], False, p == 15)],
+               ["wh0", "wh1", "wh2", "wl0", "wl1", "wl2"] + k_("y1%d" % p), k_("T"), ab, 128)
+        dl = X("dl")
+        evac("q", X("q")[:], A[:, 2], 128, k_("T"), k_("q"), ab)
+        ts(dl[:, 1:129], A[:, 1], -64.5, O.is_lt, None, None, 128, k_("T"), k_("dl"), ab)
+        ts(X("n32")[:], A[:, 1], 0.0, O.is_equal, 32.0, O.mult, 128, k_("T"), k_("n32"), ab)
+        tt(A[:, 2], A[:, 2], X("q")[:], O.subtract, 128, k_("T", "q"), k_("U"), ab)
+        scan(X("ds")[:, ::-1], T.msk[:], dl[:, 128:0:-1], O.mult, O.add, 128, ["msk"] + k_("dl"), k_("ds"), rate=0.5)
+        scan(X("d16")[:], dl[:, 0:128], T.msk[:], O.add, O.mult, 128, ["msk"] + k_("dl"), k_("d16"), rate=0.5)
+        scan(X("nb")[:], T.mmax[:], X("ds")[:], O.min, O.max, 128, ["mmax"] + k_("ds"), k_("nb"), rate=0.5)
         mats = []
-        for q in (2, 3, 0, 1):
-            dg, wt = ((T.dg2, T.W2), (T.dg3, T.W3))[q // 2]
-            mats += [(ku(q), dg[:], T.ones[:], True, False), (ku(q), wt[:], X("dl"), False, True)]
-        mm(mats, ["dg2", "dg3", "W2", "W3", "ones", k_("dl")], [k_("k%d" % q) for q in range(4)], kb, 8 * 128)
-        tt(T.x2[:, 512 * h + 256:512 * h + 512], sx(2, 2), K[:, 256:512], O.add, 256,
-           [k_("k2"), k_("k3"), k_("sl"), k_("sh")], [k_("x3")], kb)
-        ts(vp(1), X("v"), -8192.0, O.add, 0.0, O.max, 128, [k_("v")], [k_("A1")], vb)
-        ts(X("n32"), X("v"), 0.0, O.is_equal, 32.0, O.mult, 128, [k_("v")], [k_("n32")])
-        ts(vp(3), X("v"), 8191.5, O.is_gt, 77.0 * t, O.mult, 128, [k_("v")], [k_("F7")], vb)
-        tt(vp(2), vp(1), X("n32"), O.add, 128, [k_("A1"), k_("n32")], [k_("A")], vb)
-        tt(X("prod"), vp(2), zint, O.mult, 128, [k_("A")], [k_("prod")], vb, ext=ex_q)
-        tt(vp(0), vp(3), X("v"), O.add, 128, [k_("F7"), k_("v")], [k_("v0")], vb)
-        ts(X("fl"), X("prod"), 5, O.arith_shift_right, None, None, 128, [k_("prod")], [k_("fl")])
-        tt(X("sm"), vp(0), X("fl"), O.add, 128, [k_("v0"), k_("fl")], [k_("sm")], vb)
-        ts(sx(0), X("sm"), 6, O.arith_shift_right, 63, O.bitwise_and, 128, [k_("sm")], [k_("nh")])
-        ts(sx(1), X("sm"), 63, O.bitwise_and, None, None, 128, [k_("sm")], [k_("nl")])
-        tt(T.x2[:, 512 * h:512 * h + 256], sx(0, 2), K[:, 0:256], O.add, 256,
-           [k_("k0"), k_("k1"), k_("nh"), k_("nl")], [k_("x2")], kb)
+        for j in range(2):
+            mats += [(B[:, j, :, 0:16], T.i4160n[:], dl[:, 1:129], False, False), (B[:, j, :, 0:16], T.i64[:], X("d16")[:], False, False)]
+        mm(mats, ["i64", "i4160n"] + k_("d16", "dl"), k_("xq"), bb, 512)
+        mm([(B[:, j, :, 16:32], T.i64[:], X("nb")[:], False, j == 1) for j in range(2)], ["i64"] + k_("nb"), k_("xq"), bb, 256)
+        tt(X("a")[:], A[:, 2], X("n32")[:], O.max, 128, k_("U", "n32"), k_("a"), ab)
+        tt(X("prod")[:], A[:, 3], X("a")[:], O.mult, 128, k_("T", "a"), k_("prod"), ab)
+        tt(X("x2")[:, :, :, 16:32], B[:, :, :, 16:32], T.cx2[:], O.add, 256, k_("xq") + ["cx20", "cx21"], k_("x2e"), bb)
+        ts(X("fl")[:], X("prod")[:], 5, O.arith_shift_right, None, None, 128, k_("prod"), k_("fl"))
+        tt(X("sm")[:], A[:, 0], X("fl")[:], O.add, 128, k_("T", "fl"), k_("sm"), ab)
+        ts(X("nn")[:, 0:128], X("sm")[:], 6, O.arith_shift_right, 63, O.bitwise_and, 128, k_("sm"), k_("nh"))
+        ts(X("nn")[:, 128:256], X("sm")[:], 63, O.bitwise_and, None, None, 128, k_("sm"), k_("nl"))
+        tt(X("x2")[:, :, :, 0:16], B[:, :, :, 0:16], X("nn")[:], O.add, 256, k_("xq", "nh", "nl"), k_("x2r"), bb)
         if t < ROUNDS:
-            mm([(vp(1), X("dl"), T.bm[:], True, True)], ["bm", k_("dl")], [k_("A1")], vb, 128)
-            cp(X("ni"), vp(1), 128, [k_("A1")], [k_("ni")], vb)
-            ts(X("ai"), X("ni"), 1, O.bitwise_and, None, None, 128, [k_("ni")], [k_("ai")])
-            ts(X("thr"), X("ai"), -3.0, O.add, None, None, 128, [k_("ai")], [k_("thr")])
-        for i in range(16):
-            y0 = 8192 * h + 512 * i
-            ts(T.y2[:, y0:y0 + 512], T.x2[:, 512 * h:512 * h + 512], 64.0 * i, O.max, 64.0 * i + 64.0, O.min, 512,
-               [k_("x2"), k_("x3")], [k_("y2%d" % i)], rate=0.5)
-            o_ = K[:, i:128:16]
-            q = [T.y2[:, y0 + 128 * j:y0 + 128 * j + 128] for j in range(4)]
-            mm([(o_, q[0], T.w64[:], True, False), (o_, q[1], T.w1[:], False, False),
-                (o_, q[2], T.w1[:], False, False), (o_, q[3], T.w64[:], False, True)],
-               ["w64", "w1", k_("y2%d" % i)], [k_("k0")], kb, 256)
-        tt(X("nc"), ku(0), T.cc[:], O.subtract, 128, [k_("k0"), "cc"], [k_("nc")], kb)
-        mm([(ku(1), X("nc"), T.idf[:], True, True)], ["idf", k_("nc")], [k_("k1")], kb, 128)
+            ts(X("hn")[:], X("nb")[:], 257.5, O.add, None, None, 128, k_("nb"), k_("hn"), rate=0.5)
+        y2 = X("y2")
+        mm([(A[:, 0], X("d16")[:], T.i4160n[:], True, False)], ["i4160n"] + k_("d16"), k_("out"), ab, 128)
+        for s in range(16, -1, -1):
+            ts(y2[:, 256 * s:256 * s + 256], X("x2")[:, :, :, s:s + 16], 64.0 * s, O.max, 64.0 * s + 64.0, O.min, 256,
+               k_("x2e") + (k_("x2r") if s < 16 else []), k_("y2%d" % s), rate=0.5)
+            mm([(A[:, 0], y2[:, 256 * s:256 * s + 128], T.i64f[:], False, False),
+                (A[:, 0], y2[:, 256 * s + 128:256 * s + 256], T.idf[:], False, s == 0)],
+               ["i64f", "idf"] + k_("y2%d" % s), k_("out"), ab, 256)
+        base = -65.0 * 64 * 136
         if t < ROUNDS:
-            po, pf = "po%d%d" % (t, h), "pf%d%d" % (t, h)
-            ts(T[po][:], ku(1), 2048.0, O.add, None, None, 128, [k_("k1")], [po], kb)
-            act(T[pf][:], ku(1), F.Identity, 128, [k_("k1")], [pf], kb, bias=2048.0)
-            for kind, t2, hop, src in (("E", t + 1, HOPP, po), ("Z", t + 2, HOPP + HOPE, po), ("Q", t + 2, HOPP + HOPE, pf)):
-                if kind == "Z" and t2 > ROUNDS: continue
-                dst = "l%s%d%d" % (kind.lower(), t2, h)
-                sent[kind, t2, h] = send(rank + hop, T[dst][:], T[src][:], "a%s%d%d" % (kind, t2, h), [src])
-        else:
-            ts(X("fo"), ku(1), 2048.0, O.add, None, None, 128, [k_("k1")], [k_("fo")], kb)
-            send(rank + HOPP, T["lf%d" % h][:], X("fo"), "aF%d" % h, [k_("fo")])
+            po = "po%d" % t
+            ts(X(po)[:], A[:, 0], base, O.add, None, None, 128, k_("out"), k_(po), ab)
+            send(HOPP, "le%d_%d" % (t + 1, h), X(po)[:], k_(po))
+            if t + 2 <= ROUNDS: send(HOPP + HOPE, "lz%d_%d" % (t + 2, h), X(po)[:], k_(po))
+        if t + 1 >= ROUNDS:
+            pf = "pf%d" % t
+            ts(X(pf)[:], A[:, 0], base, O.add, None, None, 128, k_("out"), k_(pf), ab)
+            send(HOPP + HOPE if t < ROUNDS else HOPP, ("ly_%d" if t < ROUNDS else "lf_%d") % h, X(pf)[:], k_(pf))
 
     for t in range(1, ROUNDS + 1):
         for h in range(NC):
@@ -347,9 +362,10 @@ def rank_program(g, core, T, topo):
     succ = [[] for _ in range(n)]
     npred = [0] * n
     for i, o in enumerate(ops):
-        for d in o["d"]: succ[d].append((i, 0.0))
+        for d in o["d"]: succ[d].append((i, WAKE))
+        for d in o["k"]: succ[d].append((i, 0.0))
         for d, lag in o["a"]: succ[d].append((i, lag))
-        npred[i] = len(o["d"]) + len(o["a"])
+        npred[i] = len(o["d"]) + len(o["k"]) + len(o["a"])
     tail = [0.0] * n
     for i in range(n - 1, -1, -1):
         tail[i] = ops[i]["c"] + max([lag + tail[j] for j, lag in succ[i]] + [0.0])
@@ -368,7 +384,7 @@ def rank_program(g, core, T, topo):
         if o["e"] != "T": free[o["e"]] = end
         order.append(best)
         for j, lag in succ[best]:
-            ready[j] = max(ready[j], end + lag + WAKE)
+            ready[j] = max(ready[j], end + lag)
             npred[j] -= 1
             if npred[j] == 0: avail.append(j)
 
@@ -399,9 +415,9 @@ def rank_program(g, core, T, topo):
         if o["n"]: done[i] = (e, count[e], dict(kn))
 
     y = g.sync
-    for nm, out, land in (("aQ4%d", T.ysub, "lq4%d"), ("aF%d", T.yenz, "lf%d")):
+    for out, land in ((T.ysub, "ly_%d"), (T.yenz, "lf_%d")):
         for h in range(NC):
-            y.wait_ge(T.sem[nm % h], ARR)
+            y.wait_ge(T.sem["a" + land % h], ARR)
             y.dma_start(out[:, LN * h:LN * h + LN], T[land % h][:]).then_inc(T.sem.out, 16)
     y.wait_ge(T.sem.out, 32 * NC)
     for e in sem: y.wait_ge(sem[e], count[e])

@@ -4,7 +4,7 @@ NC = 2
 LN = 128
 ROUNDS, HOPP, HOPE = 3, 2, 5
 TK = 4
-ND = 3
+ND = 4
 CDEL, CKEEP, CPROD = (140, 0), (193, 129), {1: (0, 77), 2: (1, 91), 3: (2, 105)}
 
 SCRATCH = {
@@ -12,28 +12,28 @@ SCRATCH = {
     "ei": ("sbuf", [128, 256], "int32"), "zi": ("sbuf", [128, 256], "int32"),
     "el": ("sbuf", [128, 256], "uint16"), "zl": ("sbuf", [128, 256], "uint16"), "lz2": ("sbuf", [128, 256], "uint16"),
     "V": ("sbuf", [128, 4096], "bfloat16"), "Y": ("sbuf", [128, 4096], "bfloat16"),
-    "cm": ("sbuf", [128, 4096], "bfloat16"), "ab": ("sbuf", [128, 4096], "bfloat16"),
-    "bm": ("sbuf", [128, 8, 16], "bfloat16"), "b05": ("sbuf", [128, 2, 8], "bfloat16"), "b256": ("sbuf", [128, 8], "bfloat16"),
+    "cm": ("sbuf", [128, 32, LN], "bfloat16"), "ab": ("sbuf", [128, 32, LN], "bfloat16"),
+    "bm": ("sbuf", [128, 8, 16], "bfloat16"), "b05": ("sbuf", [128, 3, 8], "bfloat16"), "b256": ("sbuf", [128, 8], "bfloat16"),
     "wh": ("sbuf", [128, 3, 8], "float16"), "wl": ("sbuf", [128, 3, 8], "float16"),
-    "cA": ("sbuf", [128, 384], "bfloat16"), "c3": ("sbuf", [128, 4, 128], "bfloat16"), "c77": ("sbuf", [128, 3, 128], "bfloat16"),
+    "cA": ("sbuf", [128, 384], "bfloat16"), "c16": ("sbuf", [128, 128], "bfloat16"), "c77": ("sbuf", [128, 3, 128], "bfloat16"),
     "cx1": ("sbuf", [128, 3, 2, 128], "float32"), "cx2": ("sbuf", [128, 2, 128], "float32"),
     "iE1": ("sbuf", [128, 256], "bfloat16"), "iE2": ("sbuf", [128, 3, 256], "bfloat16"), "i256": ("sbuf", [128, 256], "bfloat16"),
-    "wr": ("sbuf", [128, 2, 8, 32], "bfloat16"),
+    "wr": ("sbuf", [128, 2, 128], "bfloat16"),
     "idf": ("sbuf", [128, 128], "float16"), "i64f": ("sbuf", [128, 128], "float16"),
-    "KY": ("psum", [128, 512], "float32"),
 }
 for _q in range(ND):
     SCRATCH["D%d" % _q] = ("psum", [128, 128 * TK], "float32")
-for _n in ("id1", "idn", "i63n", "i64", "i4160n", "ones", "tmp", "pio", "pk", "msk", "mmin", "mmax"):
+for _n in ("id1", "idn", "i63n", "i64", "i4160n", "ones", "tmp", "pio", "pk", "msk", "mmin", "mmax", "mone"):
     SCRATCH[_n] = ("sbuf", [128, 128], "bfloat16")
 for _h in range(NC):
-    for _n, _s, _d in (("A", [4, 8, 16], None), ("B", [2, 8, 32], None),
+    for _n, _s, _d in (("A", [4, 128], None), ("B", [4, 128], None),
                        ("R", [128], "bfloat16"), ("Sf", [128], "float16"), ("Zf", [128], "float16"),
-                       ("hE", [3, 8, 16], "bfloat16"), ("st", [128], "bfloat16"), ("w", [128], "bfloat16"),
+                       ("hE", [3, 128], "bfloat16"), ("e", [128], "bfloat16"), ("st", [128], "bfloat16"), ("w", [128], "bfloat16"),
                        ("M", [136], "bfloat16"), ("m", [136], "bfloat16"), ("nf", [128], "bfloat16"),
                        ("km", [128], "int32"), ("p0", [128], "int32"), ("pos", [128], "bfloat16"), ("wn", [128], "bfloat16"),
                        ("x1", [256], "float16"), ("y1", [4096], "float16"),
-                       ("dl", [136], "bfloat16"), ("ds", [128], "bfloat16"), ("nb", [128], "bfloat16"), ("d16", [128], "bfloat16"), ("hn", [128], "bfloat16"),
+                       ("dl", [136], "bfloat16"), ("ds", [128], "bfloat16"), ("nb", [128], "bfloat16"),
+                       ("d16", [128], "bfloat16"), ("hn", [128], "bfloat16"),
                        ("q", [128], "bfloat16"), ("n32", [128], "bfloat16"), ("a", [128], "float32"),
                        ("prod", [128], "int32"), ("fl", [128], "int32"), ("sm", [128], "int32"), ("nn", [256], "int32"),
                        ("x2", [2, 8, 32], "float16"), ("y2", [17 * 256], "float16"),
@@ -46,14 +46,11 @@ SEMAPHORES = ["cV", "cS", "cP", "cG", "lE", "lZ", "lW", "lW2", "out", "loc", "al
 for _h in range(NC):
     SEMAPHORES += ["a%s_%d" % (_k, _h) for _k in ("le2", "le3", "lz3", "ly", "lf")]
 
-CY = 0.00087
-LAG = 2.2
-VFIX, SFIX, PEC, WAKE, LEAD = 0.035, 0.065, 0.00044, 0.12, 7.0
-GATHER = 1.56
-SLACK = {"V": 0.06, "S": 0.5, "P": 0.0, "G": 0.0, "T": 0.0}
+CY, VFIX, SFIX, PEC, GATHER = 0.00083, 0.03, 0.065, 0.00043, 1.56
+WAKE, LAG, LOAD, LEAD, PASSES = 0.13, 1.6, 7.8, 5.0, 3
 GP = {"V": 2, "Y": 4}
 ONV = [("V", 1, 0, 1)] + [("Y", 1, 0, _j) for _j in range(4)]
-ONS = ()
+ONS = [(_s, ROUNDS, _h) for _s in ("hE", "pf") for _h in range(NC)]
 
 
 def rank_program(g, core, T, topo):
@@ -115,18 +112,14 @@ def rank_program(g, core, T, topo):
         return op("S", SFIX + CY * n, lambda: [S.activation(out, in_, fn, bias=bias, scale=scale)], r, w, banks)
 
     def mm(mats, r, w, banks, cyc):
-        return op("P", 0.03 + cyc * PEC, lambda: [P.matmul(o, l, q, a, z) for o, l, q, a, z in mats], r, w, banks, n=len(mats))
-
-    def evac(name, out, in_, n, r, w, banks):
-        if name in ONS: return act(out, in_, F.Copy, n, r, w, banks)
-        return cp(out, in_, n, r, w, banks)
+        return op("P", cyc * PEC, lambda: [P.matmul(o, l, q, a, z) for o, l, q, a, z in mats], r, w, banks, n=len(mats))
 
     g.sync.dma_start(T.ei[:], T.enz[:]).then_inc(T.sem.lE, 16)
     g.scalar.dma_start(T.zi[:], T.subs[:]).then_inc(T.sem.lZ, 16)
     g.sync.dma_start(T.win[:, 0:2048], T.cont[:, 0:2048]).then_inc(T.sem.lW, 16)
     g.scalar.dma_start(T.win[:, 2048:4096], T.cont[:, 2048:4096]).then_inc(T.sem.lW2, 16)
     LE, LZ, LW = [("lE", 16)], [("lZ", 16)], [("lW", 16), ("lW2", 16)]
-    t_load = op("T", 7.5, None)
+    t_load = op("T", LOAD, None)
     t_names = op("T", 2.5, None)
 
     fill(T.ones[:], 1.0, 128, ["ones"])
@@ -134,12 +127,12 @@ def rank_program(g, core, T, topo):
     def asel(out, in_, pat, cmpo, base, cm, r, w):
         return op("G", 0.4, lambda: [g.affine_select(out, in_, pat, cmpo, 0.0, base, cm)], r, w)
 
-    def iota(out, pat, w):
-        return op("G", 0.35, lambda: [g.iota(out, pat, 0, 0, allow_small_or_imprecise_dtypes=True)], (), w)
+    def iota(out, pat, base, w):
+        return op("G", 0.35, lambda: [g.iota(out, pat, base, 0, allow_small_or_imprecise_dtypes=True)], (), w)
     asel(T.id1[:], T.ones[:], [[-1, 128]], O.is_equal, 0, 1, ["ones"], ["id1"])
     asel(T.tmp[:], T.ones[:], [[-16, 8], [0, 16]], O.is_ge, 0, 1, ["ones"], ["tmp"])
     asel(T.bm[:], T.tmp[:], [[16, 8], [0, 16]], O.is_ge, 15, -1, ["tmp"], ["bm"])
-    iota(T.pio[:], [[32, 8], [1, 16]], ["pio"])
+    iota(T.pio[:], [[32, 8], [1, 16]], 0, ["pio"])
     cp(T.el[:], T.ei[:], 256, (), ["el"], ext=LE, after=[(t_names, 0.0)])
     cp(T.zl[:], T.zi[:], 256, (), ["zl"], ext=LZ, after=[(t_names, 0.0)])
 
@@ -153,9 +146,12 @@ def rank_program(g, core, T, topo):
         diag(T.iE1[:, half], (CKEEP[j] - CDEL[j]) / 32, "iE1%d" % j)
         for t in range(1, ROUNDS + 1):
             diag(T.iE2[:, t - 1, half], (CPROD[t][j] - CKEEP[j]) / 32, "iE2%d%d" % (t, j))
-        act(T.b05[:, j], T.bm[:, :, 0], F.Copy, 8, ["bm"], ["b05%d" % j], scale=0.5)
+    for j, c in enumerate((1.0, 0.5, 0.5)):
+        act(T.b05[:, j], T.bm[:, :, 0], F.Copy, 8, ["bm"], ["b05%d" % j], scale=c)
     for nm, c in (("i63n", -63.0), ("i64", 64.0), ("i4160n", -4160.0)):
         diag(T[nm][:], c, nm)
+    diag(T.wr[:, 0], 1.0, "wr0")
+    diag(T.wr[:, 1], -64.0, "wr1")
     diag(T.idf[:], 1.0, "idf", "V")
     diag(T.i64f[:], 64.0, "i64f", "V")
     act(T.b256[:], T.bm[:, :, 0], F.Copy, 8, ["bm"], ["b256"], scale=256.0)
@@ -163,23 +159,17 @@ def rank_program(g, core, T, topo):
     for j, c in enumerate((63.0, -1.0, 63.0)):
         ts(T.wh[:, j], T.bm[:, :, 0], c, O.mult, None, None, 8, ["bm"], ["wh%d" % j])
         ts(T.wl[:, j], T.bm[:, :, 0], 1.0, O.mult, None, None, 8, ["bm"], ["wl%d" % j])
-    fill(T.wr[:, :, :, 0:16], 0.0, 256, ["wr"])
-    act(T.wr[:, 0, :, 16:32], T.id1[:], F.Copy, 128, ["id1"], ["wr0"])
-    act(T.wr[:, 1, :, 16:32], T.id1[:], F.Copy, 128, ["id1"], ["wr1"], scale=-64.0)
-    for nm, c, c0 in (("msk", 1.0, 0.0), ("mmin", -1.0e7, 1.0e7), ("mmax", 1.0e7, -1.0e7)):
+    for nm, c, c0 in (("msk", 1.0, 0.0), ("mmin", -1.0e7, 1.0e7), ("mmax", 1.0e7, -1.0e7), ("mone", -2.0, 1.0)):
         fill(T[nm][:], c, 128, [nm])
         fill(T[nm][:, 0:128:16], c0, 8, [nm])
     for j, (big, small) in enumerate(((768, 3.0), (3840, 16.5), (4096, 14.5))):
         fill(T.cA[0:64, 128 * j:128 * j + 128], big / 64, 128, ["cA%d" % j])
         fill(T.cA[64:128, 128 * j:128 * j + 128], small / 64, 128, ["cA%d" % (j + 3)])
-    fill(T.cA[64:128, 0:128:16], 4.0 / 64, 8, ["cA3"])
     CA = ["cA%d" % j for j in range(6)]
-    fill(T.c3[:, 0:2], 0.0, 256, ["c30"])
-    fill(T.c3[:, 3], 16.0, 128, ["c31"])
-    iota(T.c3[:, 2], [[0, 8], [-2048, 16]], ["c32"])
-    ts(T.c3[:, 2], T.c3[:, 2], 40960.0, O.add, None, None, 128, ["c32"], ["c32"], rate=0.5)
+    fill(T.c16[:], 16.0, 128, ["c16"])
+    iota(T.c77[0:64], [[0, 24], [-4096, 16]], 81920, ["c770"])
     for t in range(1, ROUNDS + 1):
-        fill(T.c77[:, t - 1], -77.0 * t / 128, 128, ["c77%d" % t])
+        fill(T.c77[64:128, t - 1], -77.0 * t / 64, 128, ["c77%d" % t])
         for j, s in enumerate((-160, 12128)):
             c = 256 * 2112 - 2048 + s + CDEL[j] - 128 * (CPROD[t][j] - CDEL[j])
             fill(T.cx1[:, t - 1, j], float(c), 128, ["cx1%d%d" % (t, j)], rate=1.0)
@@ -187,10 +177,9 @@ def rank_program(g, core, T, topo):
     fill(T.cx2[:, 1], 12288.0, 128, ["cx21"], rate=1.0)
     for h in range(NC):
         for nm, ap, c, n, rate in (("M", T["M_%d" % h][:, 0:1], 99.0, 1, 1), ("m", T["m_%d" % h][:, 0:1], 0.0, 1, 1),
-                                   ("p0", T["p0_%d" % h][:], -1000, 128, 1),
-                                   ("dl", T["dl_%d" % h][:, 0:1], 0.0, 1, 1), ("nb", T["nb_%d" % h][:], 0.0, 128, 0.5),
-                                   ("hn", T["hn_%d" % h][:], 258.0, 128, 0.5)):
+                                   ("p0", T["p0_%d" % h][:], -1000, 128, 1), ("dl", T["dl_%d" % h][:, 0:1], 0.0, 1, 1)):
             fill(ap, c, n, [nm + str(h)], rate)
+    fill(T.tmp[:], 258.0, 128, ["tmp"])
 
     n_loc = [0]
     ARR = 8
@@ -206,7 +195,7 @@ def rank_program(g, core, T, topo):
             n_loc[0] += ARR
             g.remote_dma(T[dst][:], src, T.sem["a" + dst], T.sem.loc, pid, rid, msk)
             return []
-        sent[dst] = op("G", 0.4, f, r, (), n=0)
+        sent[dst] = op("G", 0.3, f, r, (), n=0)
 
     send(HOPE, "lz2", T.el[:], ["el"])
     dtile = [0]
@@ -214,9 +203,14 @@ def rank_program(g, core, T, topo):
     def chunk(t, h):
         X = lambda nm: T["%s_%d" % (nm, h)]
         k_ = lambda *nms: [nm + str(h) for nm in nms]
-        A, B, KY = X("A"), X("B"), T.KY
-        ab, bb, kb = k_("A"), k_("B"), ["KY"]
-        a0, a1 = LN * h, LN * h + LN
+        A, B = X("A"), X("B")
+        ab, bb = k_("A"), k_("B")
+        a0 = LN * h
+
+        def evac(name, out, in_, n, r, w, banks, add=0.0):
+            if (name, t, h) in ONS: return act(out, in_, F.Identity, n, r, w, banks, bias=add)
+            if add: return ts(out, in_, add, O.add, None, None, n, r, w, banks)
+            return cp(out, in_, n, r, w, banks)
 
         def landed(nm):
             if nm in ("el", "zl"): return T[nm], a0, [nm], [], []
@@ -236,43 +230,46 @@ def rank_program(g, core, T, topo):
             op(eng, 0.06 + 16 * n * GATHER * CY, f, r, k_(dst + "p%d" % j), ext=ext + LW, after=aft + [(t_load, 0.0)])
         for j in range(GP["Y"]): gather("Y", zb, z0, j, zr, zx, za)
         for j in range(GP["V"]): gather("V", eb, e0, j, er, ex, ea)
-        got = lambda nm: k_(*[nm + "p%d" % j for j in range(GP[nm])])
+        got = lambda nm, u: k_(*[nm + "p%d" % j for j in range(GP[nm] * u // 2, GP[nm] * (u + 1) // 2)])
         ts(X("R")[:], el, 1.0 / 64, O.mult, 159.5078125, O.add, 128, er, k_("R"), ext=ex, after=ea, rate=0.5)
         ts(X("Sf")[:], el, -2048.0, O.add, None, None, 128, er, k_("Sf"), ext=ex, after=ea, rate=0.5)
         ts(X("Zf")[:], zl, -2048.0, O.add, None, None, 128, zr, k_("Zf"), ext=zx, after=za, rate=0.5)
 
-        vs = lambda nm, k: T[nm][:, 2048 * h + k:2048 * h + 2048:16]
-        blk = lambda nm, k: T[nm][:, 2048 * h + 128 * k:2048 * h + 128 * k + 128]
+        vs = lambda nm, u, k: T[nm][:, 2048 * h + 1024 * u + k:2048 * h + 1024 * u + 1024:16]
+        blk = lambda nm, k: T[nm][:, 16 * h + k]
 
         def diffs(kind, part):
             src, dst = (("V", "cm"), ("Y", "ab"))[kind]
             d = "D%d" % (dtile[0] % ND)
             dtile[0] += 1
             D = T[d]
-            mats = []
-            for j in range(TK):
-                k = TK * part + j
-                o_ = D[:, 128 * j:128 * j + 128]
-                mats.append((o_, T.id1[:], vs(src, k), True, False))
-                mats.append((o_, T.idn[:], vs("V", (k + 1) % 16 if kind == 0 else 15), False, True))
-            mm(mats, ["id1", "idn"] + got("V") + (got("Y") if kind else []), [d], [d], 256 * TK)
-            n = 128 * TK
-            out = T[dst][:, 2048 * h + n * part:2048 * h + n * part + n]
-            act(out, D[:], F.Abs if kind else F.Sign, n, [d], k_(dst + str(part)), [d], bias=0.0 if kind else -0.5)
+            u, k0 = part // 2, 8 * (part % 2)
+            for j in range(4):
+                mats = []
+                for k in (k0 + 2 * j, k0 + 2 * j + 1):
+                    o_ = D[:, 64 * (k - k0):64 * (k - k0) + 64]
+                    mats += [(o_, T.id1[:], vs(src, u, k), True, False),
+                             (o_, T.idn[:], vs("V", u, (k + 1) % 16 if kind == 0 else 15), False, True)]
+                mm(mats, ["id1", "idn"] + got("V", u) + (got("Y", u) if kind else []), [d + str(j)], [d], 256)
+            out = T[dst][:, 16 * h + k0:16 * h + k0 + 8, 64 * u:64 * u + 64]
+            act(out, D[:], F.Abs if kind else F.Sign, 512, [d + str(j) for j in range(4)], k_(dst + str(part)), [d],
+                bias=0.0 if kind else -0.5)
 
-        mm([(A[:, 0:3], T.ones[:], T.cA[:], True, False), (A[:, 1], T.idn[:], X("nb")[:], False, False),
-            (A[:, 1], T.id1[:], X("hn")[:], False, False)], ["ones", "id1", "idn"] + CA + k_("nb", "hn"), k_("cnt"), ab, 640)
+        if t == 1:
+            mm([(A[:, 0:3], T.ones[:], T.cA[:], True, False), (A[:, 1], T.id1[:], T.tmp[:], False, False)],
+               ["ones", "id1", "tmp"] + CA, k_("cnt"), ab, 512)
+        else:
+            mm([(A[:, 0:3], T.ones[:], T.cA[:], True, False), (A[:, 1], T.idn[:], X("nb")[:], False, False),
+                (A[:, 1], T.id1[:], X("hn")[:], False, False)], ["ones", "id1", "idn"] + CA + k_("nb", "hn"), k_("cnt"), ab, 640)
         for part in range(16 // TK):
             diffs(0, part)
-            mats = []
-            for k in range(TK * part, TK * part + TK):
-                mats += [(A[:, 0, :, max(k, 1):16], blk("cm", k), T.bm[:, :, max(k, 1):16], False, False),
-                         (A[:, 1:3, :, k], blk("cm", k), T.b05[:], False, k == 15)]
-            mm(mats, ["bm", "b050", "b051"] + k_("cm%d" % part), k_("cnt"), ab,
-               sum(64 + max(64, 8 * (16 - k)) for k in range(TK * part, TK * part + TK)))
+            if part >= 2:
+                mm([(A[:, 0:3, k:128:16], blk("cm", k), T.b05[:], False, k == 15) for k in range(8 * part - 16, 8 * part - 8)],
+                   ["b050", "b051", "b052"] + k_("cm%d" % part, "cm%d" % (part - 2)), k_("cnt"), ab, 512)
         hE = X("hE")
         evac("hE", hE[:], A[:, 0:3], 384, k_("cnt"), k_("hE"), ab)
-        tt(X("st")[:], hE[:, 0], A[:, 0], O.subtract, 128, k_("cnt", "hE"), k_("st"), ab)
+        tt(X("e")[:], hE[:, 0], A[:, 0], O.subtract, 128, k_("cnt", "hE"), k_("e"), ab)
+        scan(X("st")[:], T.mone[:], X("e")[:], O.max, O.mult, 128, ["mone"] + k_("e"), k_("st"), rate=0.5)
         scan(X("w")[:], T.msk[:], X("st")[:], O.mult, O.add, 128, ["msk"] + k_("st"), k_("w"), rate=0.5)
         q1, q0 = (lambda nm: X(nm)[:, 1:129]), (lambda nm: X(nm)[:, 0:128])
         scan(q1("M"), T.mmax[:], X("w")[:], O.min, O.max, 128, ["mmax"] + k_("w"), k_("M"), rate=0.5)
@@ -281,17 +278,17 @@ def rank_program(g, core, T, topo):
             (A[:, 3], T.idn[:], q1("m"), False, False), (A[:, 3], T.id1[:], q0("m"), False, True)],
            ["id1", "idn"] + k_("M", "m"), k_("dr"), ab, 4 * 128)
         ts(X("nf")[:], A[:, 3], 0.0, O.is_equal, -32.0, O.mult, 128, k_("dr"), k_("nf"), ab)
-        mm([(KY[:, a0:a1], T.ones[:], T.pk[:], True, False)], ["ones", "pk"], k_("key"), kb, 128)
+        mm([(B[:, 3], T.ones[:], T.pk[:], True, False)], ["ones", "pk"], k_("key"), bb, 128)
         for part in range(16 // TK):
             diffs(1, part)
-            mm([(KY[:, a0 + k:a1:16], blk("ab", k), T.b256[:], False, k == 15) for k in range(TK * part, TK * part + TK)],
-               ["b256"] + k_("ab%d" % part), k_("key"), kb, 64 * TK)
-        scan(X("km")[:], T.mmin[:], KY[:, a0:a1], O.max, O.min, 128, ["mmin"] + k_("key"), k_("km"), kb)
+            if part >= 2:
+                mm([(B[:, 3, k:128:16], blk("ab", k), T.b256[:], False, k == 15) for k in range(8 * part - 16, 8 * part - 8)],
+                   ["b256"] + k_("ab%d" % part, "ab%d" % (part - 2)), k_("key"), bb, 512)
+        scan(X("km")[:], T.mmin[:], B[:, 3], O.max, O.min, 128, ["mmin"] + k_("key"), k_("km"), bb)
         ts(X("p0")[:, 0:128:16], X("km")[:, 15:128:16], 255, O.bitwise_and, None, None, 8, k_("km"), k_("p0"))
-        scan(X("pos")[:], X("p0")[:], X("st")[:], O.max, O.add, 128, k_("p0", "st"), k_("pos"), first=-1000.0)
+        scan(X("pos")[:], X("st")[:], X("p0")[:], O.add, O.max, 128, k_("p0", "st"), k_("pos"), first=-1000.0)
         ts(X("wn")[:], X("pos")[:], -1.0, O.mult, -2104.5, O.add, 128, k_("pos"), k_("wn"), rate=0.5)
-        xw = B[:, 0]
-        xh, xl = B[:, 0, 0:4], B[:, 0, 4:8]
+        xw, xh, xl = B[:, 0:2], B[:, 0], B[:, 1]
         mm([(xw, hE[:, 1], T.iE1[:], True, False), (xw, hE[:, 2], T.iE2[:, t - 1], False, False),
             (xh, T.id1[:], X("R")[:], False, False), (xl, T.i63n[:], X("R")[:], False, False),
             (xl, T.idf[:], X("Sf")[:], False, False)],
@@ -299,18 +296,18 @@ def rank_program(g, core, T, topo):
         for nm in ("nf", "pos", "wn"):
             mm([(xw, X(nm)[:], T.i256[:], False, nm == "wn")], ["i2560", "i2561"] + k_(nm), k_("xp"), bb, 256)
         tt(X("x1")[:], xw, T.cx1[:, t - 1], O.add, 256, k_("xp") + ["cx1%d0" % t, "cx1%d1" % t], k_("x1"), bb)
-        mm([(A[:], T.ones[:], T.c3[:], True, False), (A[:, 2], T.ones[:], T.c77[:, t - 1], False, False),
-            (A[:, 3], X("Zf")[:], T.idf[:], False, False)],
-           ["ones", "c30", "c31", "c32", "c77%d" % t, "idf"] + k_("Zf"), k_("T"), ab, 768)
-        mm([(B[:], X("R")[:], T.wr[:], True, False), (B[:, 1, :, 16:32], X("Sf")[:], T.idf[:], False, False)],
-           ["wr", "wr0", "wr1", "idf"] + k_("R", "Sf"), k_("xq"), bb, 640)
+        mm([(A[:, 3], T.ones[:], T.c16[:], True, False), (A[:, 3], X("Zf")[:], T.idf[:], False, False)],
+           ["ones", "c16", "idf"] + k_("Zf"), k_("T"), ab, 256)
+        mm([(B[:, 2:4], X("R")[:], T.wr[:], True, False), (B[:, 3], X("Sf")[:], T.idf[:], False, False)],
+           ["wr0", "wr1", "idf"] + k_("R", "Sf"), k_("xq"), bb, 384)
         y1 = X("y1")
         for p in range(16):
             b = 256.0 * p - 2048.0
             ts(y1[:, 256 * p:256 * p + 256], X("x1")[:], b, O.max, b + 256.0, O.min, 256, k_("x1"), k_("y1%d" % p), rate=0.5)
-            mm([(A[:, 0:3, :, p], y1[:, 256 * p:256 * p + 128], T.wh[:], False, False),
-                (A[:, 0:3, :, p], y1[:, 256 * p + 128:256 * p + 256], T.wl[:], False, p == 15)],
+            mm([(A[:, 0:3, p:128:16], y1[:, 256 * p:256 * p + 128], T.wh[:], False, False),
+                (A[:, 0:3, p:128:16], y1[:, 256 * p + 128:256 * p + 256], T.wl[:], False, False)],
                ["wh0", "wh1", "wh2", "wl0", "wl1", "wl2"] + k_("y1%d" % p), k_("T"), ab, 128)
+        mm([(A[:, 2], T.ones[:], T.c77[:, t - 1], False, True)], ["ones", "c770", "c77%d" % t], k_("T"), ab, 128)
         dl = X("dl")
         evac("q", X("q")[:], A[:, 2], 128, k_("T"), k_("q"), ab)
         ts(dl[:, 1:129], A[:, 1], -64.5, O.is_lt, None, None, 128, k_("T"), k_("dl"), ab)
@@ -321,17 +318,17 @@ def rank_program(g, core, T, topo):
         scan(X("nb")[:], T.mmax[:], X("ds")[:], O.min, O.max, 128, ["mmax"] + k_("ds"), k_("nb"), rate=0.5)
         mats = []
         for j in range(2):
-            mats += [(B[:, j, :, 0:16], T.i4160n[:], dl[:, 1:129], False, False), (B[:, j, :, 0:16], T.i64[:], X("d16")[:], False, False)]
+            mats += [(B[:, j], T.i4160n[:], dl[:, 1:129], False, False), (B[:, j], T.i64[:], X("d16")[:], False, False)]
         mm(mats, ["i64", "i4160n"] + k_("d16", "dl"), k_("xq"), bb, 512)
-        mm([(B[:, j, :, 16:32], T.i64[:], X("nb")[:], False, j == 1) for j in range(2)], ["i64"] + k_("nb"), k_("xq"), bb, 256)
+        mm([(B[:, 2 + j], T.i64[:], X("nb")[:], False, j == 1) for j in range(2)], ["i64"] + k_("nb"), k_("xq"), bb, 256)
         tt(X("a")[:], A[:, 2], X("n32")[:], O.max, 128, k_("U", "n32"), k_("a"), ab)
         tt(X("prod")[:], A[:, 3], X("a")[:], O.mult, 128, k_("T", "a"), k_("prod"), ab)
-        tt(X("x2")[:, :, :, 16:32], B[:, :, :, 16:32], T.cx2[:], O.add, 256, k_("xq") + ["cx20", "cx21"], k_("x2e"), bb)
+        tt(X("x2")[:, :, :, 16:32], B[:, 2:4], T.cx2[:], O.add, 256, k_("xq") + ["cx20", "cx21"], k_("x2e"), bb)
         ts(X("fl")[:], X("prod")[:], 5, O.arith_shift_right, None, None, 128, k_("prod"), k_("fl"))
         tt(X("sm")[:], A[:, 0], X("fl")[:], O.add, 128, k_("T", "fl"), k_("sm"), ab)
         ts(X("nn")[:, 0:128], X("sm")[:], 6, O.arith_shift_right, 63, O.bitwise_and, 128, k_("sm"), k_("nh"))
         ts(X("nn")[:, 128:256], X("sm")[:], 63, O.bitwise_and, None, None, 128, k_("sm"), k_("nl"))
-        tt(X("x2")[:, :, :, 0:16], B[:, :, :, 0:16], X("nn")[:], O.add, 256, k_("xq", "nh", "nl"), k_("x2r"), bb)
+        tt(X("x2")[:, :, :, 0:16], B[:, 0:2], X("nn")[:], O.add, 256, k_("xq", "nh", "nl"), k_("x2r"), bb)
         if t < ROUNDS:
             ts(X("hn")[:], X("nb")[:], 257.5, O.add, None, None, 128, k_("nb"), k_("hn"), rate=0.5)
         y2 = X("y2")
@@ -350,7 +347,7 @@ def rank_program(g, core, T, topo):
             if t + 2 <= ROUNDS: send(HOPP + HOPE, "lz%d_%d" % (t + 2, h), X(po)[:], k_(po))
         if t + 1 >= ROUNDS:
             pf = "pf%d" % t
-            ts(X(pf)[:], A[:, 0], base, O.add, None, None, 128, k_("out"), k_(pf), ab)
+            evac("pf", X(pf)[:], A[:, 0], 128, k_("out"), k_(pf), ab, base)
             send(HOPP + HOPE if t < ROUNDS else HOPP, ("ly_%d" if t < ROUNDS else "lf_%d") % h, X(pf)[:], k_(pf))
 
     for t in range(1, ROUNDS + 1):
@@ -359,34 +356,43 @@ def rank_program(g, core, T, topo):
             chunk(t, h)
 
     n = len(ops)
+    pred = [[(d, WAKE) for d in o["d"]] + [(d, 0.0) for d in o["k"]] + o["a"] for o in ops]
     succ = [[] for _ in range(n)]
-    npred = [0] * n
-    for i, o in enumerate(ops):
-        for d in o["d"]: succ[d].append((i, WAKE))
-        for d in o["k"]: succ[d].append((i, 0.0))
-        for d, lag in o["a"]: succ[d].append((i, lag))
-        npred[i] = len(o["d"]) + len(o["k"]) + len(o["a"])
+    for i in range(n):
+        for d, lag in pred[i]: succ[d].append((i, lag))
+
+    def place(before, after, key):
+        left = [len(b) for b in before]
+        avail = [i for i in range(n) if not left[i]]
+        end = [0.0] * n
+        taken = {}
+        while avail:
+            i = min(avail, key=key)
+            avail.remove(i)
+            c, e = ops[i]["c"], ops[i]["e"]
+            st = max([end[d] + lag for d, lag in before[i]] + [0.0])
+            if e != "T":
+                row = taken.setdefault(e, [])
+                at = 0
+                for a, b in row:
+                    if st + c <= a: break
+                    st = max(st, b)
+                    at += 1
+                row.insert(at, (st, st + c))
+            end[i] = st + c
+            for j, lag in after[i]:
+                left[j] -= 1
+                if not left[j]: avail.append(j)
+        return end
     tail = [0.0] * n
     for i in range(n - 1, -1, -1):
         tail[i] = ops[i]["c"] + max([lag + tail[j] for j, lag in succ[i]] + [0.0])
-    ready = [0.0] * n
-    avail = [i for i in range(n) if npred[i] == 0]
-    free = {}
-    order = []
-    while avail:
-        cand = [(max(ready[i], free.get(ops[i]["e"], 0.0)), i) for i in avail]
-        st, i0 = min(cand)
-        e = ops[i0]["e"]
-        best, st = min((-tail[i] - LEAD * (1 - ops[i]["h"]), i, c) for c, i in cand if ops[i]["e"] == e and c <= st + SLACK[e])[1:]
-        avail.remove(best)
-        o = ops[best]
-        end = st + o["c"]
-        if o["e"] != "T": free[o["e"]] = end
-        order.append(best)
-        for j, lag in succ[best]:
-            ready[j] = max(ready[j], end + lag)
-            npred[j] -= 1
-            if npred[j] == 0: avail.append(j)
+    end = best = place(pred, succ, lambda i: (-tail[i] + LEAD * ops[i]["h"], i))
+    for _ in range(PASSES):
+        back = place(succ, pred, lambda i: (-end[i], -i))
+        end = place(pred, succ, lambda i: (-back[i], i))
+        if max(end) < max(best): best = end
+    order = sorted(range(n), key=lambda i: (best[i] - ops[i]["c"], i))
 
     queue = {"V": V, "S": S, "P": P, "G": g}
     sem = {"V": T.sem.cV, "S": T.sem.cS, "P": T.sem.cP, "G": T.sem.cG}

from concourse.mybir import AluOpType as O, ActivationFunctionType as F

NC = 2
LN = 128
ROUNDS, HOPP, HOPE = 3, 2, 5
TK = 4
ND = 4
CDEL, CKEEP, CPROD = (140, 0), (193, 129), {1: (0, 77), 2: (1, 91), 3: (2, 105)}

SCRATCH = {
    "win": ("sbuf", [128, 4096], "bfloat16"),
    "ei": ("sbuf", [128, 256], "int32"), "zi": ("sbuf", [128, 256], "int32"),
    "el": ("sbuf", [128, 256], "uint16"), "zl": ("sbuf", [128, 256], "uint16"), "lz2": ("sbuf", [128, 256], "uint16"),
    "V": ("sbuf", [128, 4096], "bfloat16"), "Y": ("sbuf", [128, 4096], "bfloat16"),
    "cm": ("sbuf", [128, 32, LN], "bfloat16"), "ab": ("sbuf", [128, 32, LN], "bfloat16"),
    "bm": ("sbuf", [128, 8, 16], "bfloat16"), "b05": ("sbuf", [128, 3, 8], "bfloat16"), "b256": ("sbuf", [128, 8], "bfloat16"),
    "wh": ("sbuf", [128, 3, 8], "float16"), "wl": ("sbuf", [128, 3, 8], "float16"),
    "cA": ("sbuf", [128, 384], "bfloat16"), "c16": ("sbuf", [128, 128], "bfloat16"), "c77": ("sbuf", [128, 3, 128], "bfloat16"),
    "cx1": ("sbuf", [128, 3, 2, 128], "float32"), "cx2": ("sbuf", [128, 2, 128], "float32"),
    "iE1": ("sbuf", [128, 256], "bfloat16"), "iE2": ("sbuf", [128, 3, 256], "bfloat16"), "i256": ("sbuf", [128, 256], "bfloat16"),
    "wr": ("sbuf", [128, 2, 128], "bfloat16"),
    "idf": ("sbuf", [128, 128], "float16"), "i64f": ("sbuf", [128, 128], "float16"),
}
for _q in range(ND):
    SCRATCH["D%d" % _q] = ("psum", [128, 128 * TK], "float32")
for _n in ("id1", "idn", "i63n", "i64", "i4160n", "ones", "tmp", "pio", "pk", "msk", "mmin", "mmax", "mone"):
    SCRATCH[_n] = ("sbuf", [128, 128], "bfloat16")
for _h in range(NC):
    for _n, _s, _d in (("A", [4, 128], None), ("B", [4, 128], None),
                       ("R", [128], "bfloat16"), ("Sf", [128], "float16"), ("Zf", [128], "float16"),
                       ("hE", [3, 128], "bfloat16"), ("e", [128], "bfloat16"), ("st", [128], "bfloat16"), ("w", [128], "bfloat16"),
                       ("M", [136], "bfloat16"), ("m", [136], "bfloat16"), ("nf", [128], "bfloat16"),
                       ("km", [128], "int32"), ("p0", [128], "int32"), ("pos", [128], "bfloat16"), ("wn", [128], "bfloat16"),
                       ("x1", [256], "float16"), ("y1", [4096], "float16"),
                       ("dl", [136], "bfloat16"), ("ds", [128], "bfloat16"), ("nb", [128], "bfloat16"),
                       ("d16", [128], "bfloat16"), ("hn", [128], "bfloat16"),
                       ("q", [128], "bfloat16"), ("n32", [128], "bfloat16"), ("a", [128], "float32"),
                       ("prod", [128], "int32"), ("fl", [128], "int32"), ("sm", [128], "int32"), ("nn", [256], "int32"),
                       ("x2", [2, 8, 32], "float16"), ("y2", [17 * 256], "float16"),
                       ("le2", [LN], "uint16"), ("le3", [LN], "uint16"), ("lz3", [LN], "uint16"),
                       ("ly", [LN], "float32"), ("lf", [LN], "float32"),
                       ("po1", [LN], "uint16"), ("po2", [LN], "uint16"), ("pf2", [LN], "float32"), ("pf3", [LN], "float32")):
        SCRATCH["%s_%d" % (_n, _h)] = ("sbuf", [128] + _s, _d) if _d else ("psum", [128] + _s, "float32")

SEMAPHORES = ["cV", "cS", "cP", "cG", "lE", "lZ", "lW", "lW2", "out", "loc", "alz2"]
for _h in range(NC):
    SEMAPHORES += ["a%s_%d" % (_k, _h) for _k in ("le2", "le3", "lz3", "ly", "lf")]

CY, VFIX, SFIX, PEC, GATHER = 0.00083, 0.03, 0.065, 0.00043, 1.56
WAKE, LAG, LOAD, LEAD, PASSES = 0.13, 1.6, 7.8, 5.0, 3
GP = {"V": 2, "Y": 4}
ONV = [("V", 1, 0, 1)] + [("Y", 1, 0, _j) for _j in range(4)]
ONS = [(_s, ROUNDS, _h) for _s in ("hE", "pf") for _h in range(NC)]


def rank_program(g, core, T, topo):
    rank = T.rank_of(core)
    if rank is None:
        return
    n_ranks = len(T.cores)
    V, S, P = g.vector, g.scalar, g.tensor
    ops, cur = [], [0]
    lastw, readers, bank = {}, {}, {}

    def op(eng, cost, fn, reads=(), writes=(), banks=(), ext=(), after=(), n=1):
        i = len(ops)
        deps = set()
        for r in reads:
            if r in lastw: deps.add(lastw[r])
            readers.setdefault(r, []).append(i)
        for w in writes:
            if w in lastw: deps.add(lastw[w])
            for q in readers.get(w, []):
                if q != i: deps.add(q)
            lastw[w] = i
            readers[w] = []
        keep = set()
        for b in banks:
            if b not in bank: bank[b] = [eng, [], []]
            if bank[b][0] != eng: bank[b] = [eng, bank[b][2], []]
            deps.update(bank[b][1])
            if eng == "P" and bank[b][2]: keep.add(bank[b][2][-1])
            bank[b][2].append(i)
        if eng == "P":
            keep.update(d for d in deps if ops[d]["e"] == "P")
            deps = {d for d in deps if ops[d]["e"] != "P"}
        ops.append({"e": eng, "c": cost, "f": fn, "d": deps, "k": keep, "x": list(ext), "a": list(after), "n": n, "h": cur[0]})
        return i

    def cv(n, rate=1.0):
        return VFIX + CY * max(64.0, n * rate)

    def ts(out, in0, s1, o0, s2, o1, n, r, w, banks=(), ext=(), after=(), rate=1.0):
        def f():
            if o1 is None: return [V.tensor_scalar(out, in0, s1, None, o0)]
            return [V.tensor_scalar(out, in0, s1, s2, o0, o1)]
        return op("V", cv(n, rate), f, r, w, banks, ext, after)

    def tt(out, a, b, o, n, r, w, banks=()):
        return op("V", cv(n), lambda: [V.tensor_tensor(out, a, b, o)], r, w, banks)

    def cp(out, a, n, r, w, banks=(), ext=(), after=(), rate=1.0):
        return op("V", cv(n, rate), lambda: [V.tensor_copy(out, a)], r, w, banks, ext, after)

    def fill(ap, c, n, w, rate=0.5):
        return op("V", cv(n, rate), lambda: [V.memset(ap, c)], (), w)

    def scan(out, d0, d1, o0, o1, n, r, w, banks=(), rate=1.0, first=0.0):
        return op("V", cv(n, rate), lambda: [V.tensor_tensor_scan(out, d0, d1, first, o0, o1)], r, w, banks)

    def act(out, in_, fn, n, r, w, banks=(), bias=0.0, scale=1.0):
        return op("S", SFIX + CY * n, lambda: [S.activation(out, in_, fn, bias=bias, scale=scale)], r, w, banks)

    def mm(mats, r, w, banks, cyc):
        return op("P", cyc * PEC, lambda: [P.matmul(o, l, q, a, z) for o, l, q, a, z in mats], r, w, banks, n=len(mats))

    g.sync.dma_start(T.ei[:], T.enz[:]).then_inc(T.sem.lE, 16)
    g.scalar.dma_start(T.zi[:], T.subs[:]).then_inc(T.sem.lZ, 16)
    g.sync.dma_start(T.win[:, 0:2048], T.cont[:, 0:2048]).then_inc(T.sem.lW, 16)
    g.scalar.dma_start(T.win[:, 2048:4096], T.cont[:, 2048:4096]).then_inc(T.sem.lW2, 16)
    LE, LZ, LW = [("lE", 16)], [("lZ", 16)], [("lW", 16), ("lW2", 16)]
    t_load = op("T", LOAD, None)
    t_names = op("T", 2.5, None)

    fill(T.ones[:], 1.0, 128, ["ones"])

    def asel(out, in_, pat, cmpo, base, cm, r, w):
        return op("G", 0.4, lambda: [g.affine_select(out, in_, pat, cmpo, 0.0, base, cm)], r, w)

    def iota(out, pat, base, w):
        return op("G", 0.35, lambda: [g.iota(out, pat, base, 0, allow_small_or_imprecise_dtypes=True)], (), w)
    asel(T.id1[:], T.ones[:], [[-1, 128]], O.is_equal, 0, 1, ["ones"], ["id1"])
    asel(T.tmp[:], T.ones[:], [[-16, 8], [0, 16]], O.is_ge, 0, 1, ["ones"], ["tmp"])
    asel(T.bm[:], T.tmp[:], [[16, 8], [0, 16]], O.is_ge, 15, -1, ["tmp"], ["bm"])
    iota(T.pio[:], [[32, 8], [1, 16]], 0, ["pio"])
    cp(T.el[:], T.ei[:], 256, (), ["el"], ext=LE, after=[(t_names, 0.0)])
    cp(T.zl[:], T.zi[:], 256, (), ["zl"], ext=LZ, after=[(t_names, 0.0)])

    def diag(out, c, w, eng="S"):
        if eng == "S": act(out, T.id1[:], F.Copy, 128, ["id1"], [w], scale=c)
        else: ts(out, T.id1[:], c, O.mult, None, None, 128, ["id1"], [w], rate=0.5)
    diag(T.idn[:], -1.0, "idn")
    for j in range(2):
        half = slice(128 * j, 128 * j + 128)
        diag(T.i256[:, half], 256.0, "i256%d" % j)
        diag(T.iE1[:, half], (CKEEP[j] - CDEL[j]) / 32, "iE1%d" % j)
        for t in range(1, ROUNDS + 1):
            diag(T.iE2[:, t - 1, half], (CPROD[t][j] - CKEEP[j]) / 32, "iE2%d%d" % (t, j))
    for j, c in enumerate((1.0, 0.5, 0.5)):
        act(T.b05[:, j], T.bm[:, :, 0], F.Copy, 8, ["bm"], ["b05%d" % j], scale=c)
    for nm, c in (("i63n", -63.0), ("i64", 64.0), ("i4160n", -4160.0)):
        diag(T[nm][:], c, nm)
    diag(T.wr[:, 0], 1.0, "wr0")
    diag(T.wr[:, 1], -64.0, "wr1")
    diag(T.idf[:], 1.0, "idf", "V")
    diag(T.i64f[:], 64.0, "i64f", "V")
    act(T.b256[:], T.bm[:, :, 0], F.Copy, 8, ["bm"], ["b256"], scale=256.0)
    act(T.pk[:], T.pio[:], F.Copy, 128, ["pio"], ["pk"], scale=1.0 / 128)
    for j, c in enumerate((63.0, -1.0, 63.0)):
        ts(T.wh[:, j], T.bm[:, :, 0], c, O.mult, None, None, 8, ["bm"], ["wh%d" % j])
        ts(T.wl[:, j], T.bm[:, :, 0], 1.0, O.mult, None, None, 8, ["bm"], ["wl%d" % j])
    for nm, c, c0 in (("msk", 1.0, 0.0), ("mmin", -1.0e7, 1.0e7), ("mmax", 1.0e7, -1.0e7), ("mone", -2.0, 1.0)):
        fill(T[nm][:], c, 128, [nm])
        fill(T[nm][:, 0:128:16], c0, 8, [nm])
    for j, (big, small) in enumerate(((768, 3.0), (3840, 16.5), (4096, 14.5))):
        fill(T.cA[0:64, 128 * j:128 * j + 128], big / 64, 128, ["cA%d" % j])
        fill(T.cA[64:128, 128 * j:128 * j + 128], small / 64, 128, ["cA%d" % (j + 3)])
    CA = ["cA%d" % j for j in range(6)]
    fill(T.c16[:], 16.0, 128, ["c16"])
    iota(T.c77[0:64], [[0, 24], [-4096, 16]], 81920, ["c770"])
    for t in range(1, ROUNDS + 1):
        fill(T.c77[64:128, t - 1], -77.0 * t / 64, 128, ["c77%d" % t])
        for j, s in enumerate((-160, 12128)):
            c = 256 * 2112 - 2048 + s + CDEL[j] - 128 * (CPROD[t][j] - CDEL[j])
            fill(T.cx1[:, t - 1, j], float(c), 128, ["cx1%d%d" % (t, j)], rate=1.0)
    fill(T.cx2[:, 0], -160.0, 128, ["cx20"], rate=1.0)
    fill(T.cx2[:, 1], 12288.0, 128, ["cx21"], rate=1.0)
    for h in range(NC):
        for nm, ap, c, n, rate in (("M", T["M_%d" % h][:, 0:1], 99.0, 1, 1), ("m", T["m_%d" % h][:, 0:1], 0.0, 1, 1),
                                   ("p0", T["p0_%d" % h][:], -1000, 128, 1), ("dl", T["dl_%d" % h][:, 0:1], 0.0, 1, 1)):
            fill(ap, c, n, [nm + str(h)], rate)
    fill(T.tmp[:], 258.0, 128, ["tmp"])

    n_loc = [0]
    ARR = 8
    sent = {}

    def send(hop, dst, src, r):
        to = T.cores[(rank + hop) % n_ranks]

        def f():
            msk = 0
            for e in topo.engines(core, to)[:ARR]: msk |= 1 << e
            rid, pid = topo.addr(to)[:2]
            n_loc[0] += ARR
            g.remote_dma(T[dst][:], src, T.sem["a" + dst], T.sem.loc, pid, rid, msk)
            return []
        sent[dst] = op("G", 0.3, f, r, (), n=0)

    send(HOPE, "lz2", T.el[:], ["el"])
    dtile = [0]

    def chunk(t, h):
        X = lambda nm: T["%s_%d" % (nm, h)]
        k_ = lambda *nms: [nm + str(h) for nm in nms]
        A, B = X("A"), X("B")
        ab, bb = k_("A"), k_("B")
        a0 = LN * h

        def evac(name, out, in_, n, r, w, banks, add=0.0):
            if (name, t, h) in ONS: return act(out, in_, F.Identity, n, r, w, banks, bias=add)
            if add: return ts(out, in_, add, O.add, None, None, n, r, w, banks)
            return cp(out, in_, n, r, w, banks)

        def landed(nm):
            if nm in ("el", "zl"): return T[nm], a0, [nm], [], []
            if nm == "lz2": return T.lz2, a0, [], [("alz2", ARR)], [(sent[nm], LAG)]
            nm = "%s_%d" % (nm, h)
            return T[nm], 0, [], [("a" + nm, ARR)], [(sent[nm], LAG)]
        eb, e0, er, ex, ea = landed("el" if t == 1 else "le%d" % t)
        zb, z0, zr, zx, za = landed("zl" if t == 1 else "lz%d" % t)
        el, zl = eb[:, e0:e0 + LN], zb[:, z0:z0 + LN]

        def gather(dst, buf, c0, j, r, ext, aft):
            n = LN // GP[dst]
            o_ = T[dst][:, 2048 * h + 16 * n * j:2048 * h + 16 * n * (j + 1)]
            w_ = T.win[:, 0:4096].indirect(buf[:, c0 + n * j:c0 + n * (j + 1)])
            eng = "V" if (dst, t, h, j) in ONV else "S"
            f = (lambda: [S.activation(o_, w_, F.Copy)]) if eng == "S" else (lambda: [V.tensor_copy(o_, w_)])
            op(eng, 0.06 + 16 * n * GATHER * CY, f, r, k_(dst + "p%d" % j), ext=ext + LW, after=aft + [(t_load, 0.0)])
        for j in range(GP["Y"]): gather("Y", zb, z0, j, zr, zx, za)
        for j in range(GP["V"]): gather("V", eb, e0, j, er, ex, ea)
        got = lambda nm, u: k_(*[nm + "p%d" % j for j in range(GP[nm] * u // 2, GP[nm] * (u + 1) // 2)])
        ts(X("R")[:], el, 1.0 / 64, O.mult, 159.5078125, O.add, 128, er, k_("R"), ext=ex, after=ea, rate=0.5)
        ts(X("Sf")[:], el, -2048.0, O.add, None, None, 128, er, k_("Sf"), ext=ex, after=ea, rate=0.5)
        ts(X("Zf")[:], zl, -2048.0, O.add, None, None, 128, zr, k_("Zf"), ext=zx, after=za, rate=0.5)

        vs = lambda nm, u, k: T[nm][:, 2048 * h + 1024 * u + k:2048 * h + 1024 * u + 1024:16]
        blk = lambda nm, k: T[nm][:, 16 * h + k]

        def diffs(kind, part):
            src, dst = (("V", "cm"), ("Y", "ab"))[kind]
            d = "D%d" % (dtile[0] % ND)
            dtile[0] += 1
            D = T[d]
            u, k0 = part // 2, 8 * (part % 2)
            for j in range(4):
                mats = []
                for k in (k0 + 2 * j, k0 + 2 * j + 1):
                    o_ = D[:, 64 * (k - k0):64 * (k - k0) + 64]
                    mats += [(o_, T.id1[:], vs(src, u, k), True, False),
                             (o_, T.idn[:], vs("V", u, (k + 1) % 16 if kind == 0 else 15), False, True)]
                mm(mats, ["id1", "idn"] + got("V", u) + (got("Y", u) if kind else []), [d + str(j)], [d], 256)
            out = T[dst][:, 16 * h + k0:16 * h + k0 + 8, 64 * u:64 * u + 64]
            act(out, D[:], F.Abs if kind else F.Sign, 512, [d + str(j) for j in range(4)], k_(dst + str(part)), [d],
                bias=0.0 if kind else -0.5)

        if t == 1:
            mm([(A[:, 0:3], T.ones[:], T.cA[:], True, False), (A[:, 1], T.id1[:], T.tmp[:], False, False)],
               ["ones", "id1", "tmp"] + CA, k_("cnt"), ab, 512)
        else:
            mm([(A[:, 0:3], T.ones[:], T.cA[:], True, False), (A[:, 1], T.idn[:], X("nb")[:], False, False),
                (A[:, 1], T.id1[:], X("hn")[:], False, False)], ["ones", "id1", "idn"] + CA + k_("nb", "hn"), k_("cnt"), ab, 640)
        for part in range(16 // TK):
            diffs(0, part)
            if part >= 2:
                mm([(A[:, 0:3, k:128:16], blk("cm", k), T.b05[:], False, k == 15) for k in range(8 * part - 16, 8 * part - 8)],
                   ["b050", "b051", "b052"] + k_("cm%d" % part, "cm%d" % (part - 2)), k_("cnt"), ab, 512)
        hE = X("hE")
        evac("hE", hE[:], A[:, 0:3], 384, k_("cnt"), k_("hE"), ab)
        tt(X("e")[:], hE[:, 0], A[:, 0], O.subtract, 128, k_("cnt", "hE"), k_("e"), ab)
        scan(X("st")[:], T.mone[:], X("e")[:], O.max, O.mult, 128, ["mone"] + k_("e"), k_("st"), rate=0.5)
        scan(X("w")[:], T.msk[:], X("st")[:], O.mult, O.add, 128, ["msk"] + k_("st"), k_("w"), rate=0.5)
        q1, q0 = (lambda nm: X(nm)[:, 1:129]), (lambda nm: X(nm)[:, 0:128])
        scan(q1("M"), T.mmax[:], X("w")[:], O.min, O.max, 128, ["mmax"] + k_("w"), k_("M"), rate=0.5)
        scan(q1("m"), T.mmin[:], X("w")[:], O.max, O.min, 128, ["mmin"] + k_("w"), k_("m"), rate=0.5)
        mm([(A[:, 3], T.id1[:], q1("M"), True, False), (A[:, 3], T.idn[:], q0("M"), False, False),
            (A[:, 3], T.idn[:], q1("m"), False, False), (A[:, 3], T.id1[:], q0("m"), False, True)],
           ["id1", "idn"] + k_("M", "m"), k_("dr"), ab, 4 * 128)
        ts(X("nf")[:], A[:, 3], 0.0, O.is_equal, -32.0, O.mult, 128, k_("dr"), k_("nf"), ab)
        mm([(B[:, 3], T.ones[:], T.pk[:], True, False)], ["ones", "pk"], k_("key"), bb, 128)
        for part in range(16 // TK):
            diffs(1, part)
            if part >= 2:
                mm([(B[:, 3, k:128:16], blk("ab", k), T.b256[:], False, k == 15) for k in range(8 * part - 16, 8 * part - 8)],
                   ["b256"] + k_("ab%d" % part, "ab%d" % (part - 2)), k_("key"), bb, 512)
        scan(X("km")[:], T.mmin[:], B[:, 3], O.max, O.min, 128, ["mmin"] + k_("key"), k_("km"), bb)
        ts(X("p0")[:, 0:128:16], X("km")[:, 15:128:16], 255, O.bitwise_and, None, None, 8, k_("km"), k_("p0"))
        scan(X("pos")[:], X("st")[:], X("p0")[:], O.add, O.max, 128, k_("p0", "st"), k_("pos"), first=-1000.0)
        ts(X("wn")[:], X("pos")[:], -1.0, O.mult, -2104.5, O.add, 128, k_("pos"), k_("wn"), rate=0.5)
        xw, xh, xl = B[:, 0:2], B[:, 0], B[:, 1]
        mm([(xw, hE[:, 1], T.iE1[:], True, False), (xw, hE[:, 2], T.iE2[:, t - 1], False, False),
            (xh, T.id1[:], X("R")[:], False, False), (xl, T.i63n[:], X("R")[:], False, False),
            (xl, T.idf[:], X("Sf")[:], False, False)],
           ["iE10", "iE11", "iE2%d0" % t, "iE2%d1" % t, "id1", "i63n", "idf"] + k_("hE", "R", "Sf"), k_("xp"), bb, 7 * 128)
        for nm in ("nf", "pos", "wn"):
            mm([(xw, X(nm)[:], T.i256[:], False, nm == "wn")], ["i2560", "i2561"] + k_(nm), k_("xp"), bb, 256)
        tt(X("x1")[:], xw, T.cx1[:, t - 1], O.add, 256, k_("xp") + ["cx1%d0" % t, "cx1%d1" % t], k_("x1"), bb)
        mm([(A[:, 3], T.ones[:], T.c16[:], True, False), (A[:, 3], X("Zf")[:], T.idf[:], False, False)],
           ["ones", "c16", "idf"] + k_("Zf"), k_("T"), ab, 256)
        mm([(B[:, 2:4], X("R")[:], T.wr[:], True, False), (B[:, 3], X("Sf")[:], T.idf[:], False, False)],
           ["wr0", "wr1", "idf"] + k_("R", "Sf"), k_("xq"), bb, 384)
        y1 = X("y1")
        for p in range(16):
            b = 256.0 * p - 2048.0
            ts(y1[:, 256 * p:256 * p + 256], X("x1")[:], b, O.max, b + 256.0, O.min, 256, k_("x1"), k_("y1%d" % p), rate=0.5)
            mm([(A[:, 0:3, p:128:16], y1[:, 256 * p:256 * p + 128], T.wh[:], False, False),
                (A[:, 0:3, p:128:16], y1[:, 256 * p + 128:256 * p + 256], T.wl[:], False, False)],
               ["wh0", "wh1", "wh2", "wl0", "wl1", "wl2"] + k_("y1%d" % p), k_("T"), ab, 128)
        mm([(A[:, 2], T.ones[:], T.c77[:, t - 1], False, True)], ["ones", "c770", "c77%d" % t], k_("T"), ab, 128)
        dl = X("dl")
        evac("q", X("q")[:], A[:, 2], 128, k_("T"), k_("q"), ab)
        ts(dl[:, 1:129], A[:, 1], -64.5, O.is_lt, None, None, 128, k_("T"), k_("dl"), ab)
        ts(X("n32")[:], A[:, 1], 0.0, O.is_equal, 32.0, O.mult, 128, k_("T"), k_("n32"), ab)
        tt(A[:, 2], A[:, 2], X("q")[:], O.subtract, 128, k_("T", "q"), k_("U"), ab)
        scan(X("ds")[:, ::-1], T.msk[:], dl[:, 128:0:-1], O.mult, O.add, 128, ["msk"] + k_("dl"), k_("ds"), rate=0.5)
        scan(X("d16")[:], dl[:, 0:128], T.msk[:], O.add, O.mult, 128, ["msk"] + k_("dl"), k_("d16"), rate=0.5)
        scan(X("nb")[:], T.mmax[:], X("ds")[:], O.min, O.max, 128, ["mmax"] + k_("ds"), k_("nb"), rate=0.5)
        mats = []
        for j in range(2):
            mats += [(B[:, j], T.i4160n[:], dl[:, 1:129], False, False), (B[:, j], T.i64[:], X("d16")[:], False, False)]
        mm(mats, ["i64", "i4160n"] + k_("d16", "dl"), k_("xq"), bb, 512)
        mm([(B[:, 2 + j], T.i64[:], X("nb")[:], False, j == 1) for j in range(2)], ["i64"] + k_("nb"), k_("xq"), bb, 256)
        tt(X("a")[:], A[:, 2], X("n32")[:], O.max, 128, k_("U", "n32"), k_("a"), ab)
        tt(X("prod")[:], A[:, 3], X("a")[:], O.mult, 128, k_("T", "a"), k_("prod"), ab)
        tt(X("x2")[:, :, :, 16:32], B[:, 2:4], T.cx2[:], O.add, 256, k_("xq") + ["cx20", "cx21"], k_("x2e"), bb)
        ts(X("fl")[:], X("prod")[:], 5, O.arith_shift_right, None, None, 128, k_("prod"), k_("fl"))
        tt(X("sm")[:], A[:, 0], X("fl")[:], O.add, 128, k_("T", "fl"), k_("sm"), ab)
        ts(X("nn")[:, 0:128], X("sm")[:], 6, O.arith_shift_right, 63, O.bitwise_and, 128, k_("sm"), k_("nh"))
        ts(X("nn")[:, 128:256], X("sm")[:], 63, O.bitwise_and, None, None, 128, k_("sm"), k_("nl"))
        tt(X("x2")[:, :, :, 0:16], B[:, 0:2], X("nn")[:], O.add, 256, k_("xq", "nh", "nl"), k_("x2r"), bb)
        if t < ROUNDS:
            ts(X("hn")[:], X("nb")[:], 257.5, O.add, None, None, 128, k_("nb"), k_("hn"), rate=0.5)
        y2 = X("y2")
        mm([(A[:, 0], X("d16")[:], T.i4160n[:], True, False)], ["i4160n"] + k_("d16"), k_("out"), ab, 128)
        for s in range(16, -1, -1):
            ts(y2[:, 256 * s:256 * s + 256], X("x2")[:, :, :, s:s + 16], 64.0 * s, O.max, 64.0 * s + 64.0, O.min, 256,
               k_("x2e") + (k_("x2r") if s < 16 else []), k_("y2%d" % s), rate=0.5)
            mm([(A[:, 0], y2[:, 256 * s:256 * s + 128], T.i64f[:], False, False),
                (A[:, 0], y2[:, 256 * s + 128:256 * s + 256], T.idf[:], False, s == 0)],
               ["i64f", "idf"] + k_("y2%d" % s), k_("out"), ab, 256)
        base = -65.0 * 64 * 136
        if t < ROUNDS:
            po = "po%d" % t
            ts(X(po)[:], A[:, 0], base, O.add, None, None, 128, k_("out"), k_(po), ab)
            send(HOPP, "le%d_%d" % (t + 1, h), X(po)[:], k_(po))
            if t + 2 <= ROUNDS: send(HOPP + HOPE, "lz%d_%d" % (t + 2, h), X(po)[:], k_(po))
        if t + 1 >= ROUNDS:
            pf = "pf%d" % t
            evac("pf", X(pf)[:], A[:, 0], 128, k_("out"), k_(pf), ab, base)
            send(HOPP + HOPE if t < ROUNDS else HOPP, ("ly_%d" if t < ROUNDS else "lf_%d") % h, X(pf)[:], k_(pf))

    for t in range(1, ROUNDS + 1):
        for h in range(NC):
            cur[0] = h
            chunk(t, h)

    n = len(ops)
    pred = [[(d, WAKE) for d in o["d"]] + [(d, 0.0) for d in o["k"]] + o["a"] for o in ops]
    succ = [[] for _ in range(n)]
    for i in range(n):
        for d, lag in pred[i]: succ[d].append((i, lag))

    def place(before, after, key):
        left = [len(b) for b in before]
        avail = [i for i in range(n) if not left[i]]
        end = [0.0] * n
        taken = {}
        while avail:
            i = min(avail, key=key)
            avail.remove(i)
            c, e = ops[i]["c"], ops[i]["e"]
            st = max([end[d] + lag for d, lag in before[i]] + [0.0])
            if e != "T":
                row = taken.setdefault(e, [])
                at = 0
                for a, b in row:
                    if st + c <= a: break
                    st = max(st, b)
                    at += 1
                row.insert(at, (st, st + c))
            end[i] = st + c
            for j, lag in after[i]:
                left[j] -= 1
                if not left[j]: avail.append(j)
        return end
    tail = [0.0] * n
    for i in range(n - 1, -1, -1):
        tail[i] = ops[i]["c"] + max([lag + tail[j] for j, lag in succ[i]] + [0.0])
    end = best = place(pred, succ, lambda i: (-tail[i] + LEAD * ops[i]["h"], i))
    for _ in range(PASSES):
        back = place(succ, pred, lambda i: (-end[i], -i))
        end = place(pred, succ, lambda i: (-back[i], i))
        if max(end) < max(best): best = end
    order = sorted(range(n), key=lambda i: (best[i] - ops[i]["c"], i))

    queue = {"V": V, "S": S, "P": P, "G": g}
    sem = {"V": T.sem.cV, "S": T.sem.cS, "P": T.sem.cP, "G": T.sem.cG}
    count = {"V": 0, "S": 0, "P": 0, "G": 0}
    known = {e: {} for e in queue}
    done = {}
    for i in order:
        o = ops[i]
        e = o["e"]
        if e == "T": continue
        kn = known[e]
        for d in sorted(o["d"], key=lambda d: -done[d][1]):
            e2, c2, snap = done[d]
            if kn.get(e2, 0) >= c2: continue
            queue[e].wait_ge(sem[e2], c2)
            for a, b in snap.items():
                if kn.get(a, 0) < b: kn[a] = b
            kn[e2] = c2
        for nm, val in o["x"]:
            if kn.get(nm, 0) >= val: continue
            queue[e].wait_ge(T.sem[nm], val)
            kn[nm] = val
        for ins in o["f"]():
            ins.then_inc(sem[e], 1)
            count[e] += 1
        if o["n"]: done[i] = (e, count[e], dict(kn))

    y = g.sync
    for out, land in ((T.ysub, "ly_%d"), (T.yenz, "lf_%d")):
        for h in range(NC):
            y.wait_ge(T.sem["a" + land % h], ARR)
            y.dma_start(out[:, LN * h:LN * h + LN], T[land % h][:]).then_inc(T.sem.out, 16)
    y.wait_ge(T.sem.out, 32 * NC)
    for e in sem: y.wait_ge(sem[e], count[e])
    g.wait_ge(T.sem.loc, n_loc[0])
